import numpy as np
import ml_dtypes


def mxq(x, axis, fmt="e4m3"):
    dtype, down = {"e4m3": (ml_dtypes.float8_e4m3fn, 7), "e5m2": (ml_dtypes.float8_e5m2, 14)}[fmt]
    v = np.moveaxis(np.asarray(x, np.float32).astype(ml_dtypes.bfloat16).astype(np.float64), axis, -1)
    blocks = v.reshape(v.shape[:-1] + (-1, 32))
    amax = np.abs(blocks).max(-1, keepdims=True)
    byte = np.maximum(np.where(amax > 0, np.frexp(amax)[1] - 1 + 127, 0) - down, 1)
    scale = np.exp2(byte - 127.0)
    codes = (blocks / scale).astype(np.float32).astype(dtype).astype(np.float64)
    return np.moveaxis((codes * scale).reshape(v.shape), -1, axis)


WIDE = False


def mx_kscale(k):
    if not WIDE:
        return np.ones(k)
    levels = np.array([10, -10, 5, -5, 0])
    if k % 512:
        return np.exp2(np.random.permutation(np.resize(levels, k // 32))).repeat(32)
    a = np.empty((k // 512, 16))
    for p in range(k // 512):
        a[p, :8] = np.random.permutation(np.resize(levels, 8))
        for g in range(8):
            far = levels[np.abs(levels - a[p, g]) >= 10]
            a[p, g + 8] = far[np.random.randint(len(far))]
    return np.exp2(a.ravel()).repeat(32)


BF16 = ml_dtypes.bfloat16


def bf(x):
    return np.asarray(x, np.float32).astype(BF16)


def f64(x):
    return np.asarray(x).astype(np.float64)

E4M3FN = np.array([(-1.0 if i & 128 else 1.0) * ((1.0 + (i & 7) / 8.0) * 2.0 ** (((i >> 3) & 15) - 7) if i & 120 else (i & 7) * 2.0 ** -9) for i in range(256)])


def e4m3fn_bytes(y):
    return np.clip(np.asarray(y, np.float64), -448.0, 448.0).astype(np.float32).astype(ml_dtypes.float8_e4m3fn).view(np.uint8)


def e4m3fn_values(b):
    return E4M3FN[b]

def planes(Y):
    n, m = Y.shape
    b = f64(bf(Y)).reshape(n // 32, 32, m)
    amax = np.abs(b).max(1)
    byte = np.clip(np.where(amax > 0, np.frexp(amax)[1] - 1 + 127 - 7, 1), 1, 254)
    codes = (b * np.exp2(127.0 - byte)[:, None, :]).reshape(n, m).astype(np.float32).astype(ml_dtypes.float8_e4m3fn).view(np.uint8)
    words = codes.reshape(n // 512, 128, 4, m).transpose(0, 1, 3, 2)
    return np.ascontiguousarray(words), np.ascontiguousarray(byte.astype(np.uint8).reshape(n // 512, 16, m))


A, F, T, BLK = 2048, 1024, 1024, 128
E4M3_MAX = 448.0


def setup_inputs():
    qa = mx_kscale(A)
    pf = mx_kscale(F)
    amp = np.exp(0.8 * np.random.randn(A))
    D = np.random.randn(A, F) / np.sqrt(A) * qa[:, None] * pf[None, :]
    D_scale = (np.abs(D).reshape(A, F // BLK, BLK).max(axis=2) / E4M3_MAX).astype(np.float32)
    D_bytes = e4m3fn_bytes(D / np.repeat(f64(D_scale), BLK, axis=1))
    Z = bf(np.random.randn(T, A) * amp)
    c = bf((np.exp(0.3 * np.random.randn(A)) / amp / qa)[None, :])
    X = bf(np.random.randn(T, F) * pf)
    w = bf((np.exp(0.3 * np.random.randn(F)) / pf / pf)[None, :])
    e = bf((0.5 * amp * np.exp(0.3 * np.random.randn(A)) / qa)[None, :])
    theta = bf((0.15 * amp * np.exp(0.2 * np.random.randn(A)))[None, :])
    return {"Z": Z, "c": c, "D_bytes": D_bytes, "D_scale": D_scale,
            "X": X, "w": w, "e": e, "theta": theta}


def reference(Z, c, D_bytes, D_scale, X, w, e, theta):
    D = e4m3fn_values(D_bytes) * np.repeat(f64(D_scale), BLK, axis=1)
    V = f64(Z) * f64(c)
    H = mxq(V, 1, "e4m3") @ mxq(D, 0, "e4m3")
    R = (f64(X) - H) * f64(w)
    G = mxq(R, 1, "e4m3") @ mxq(D, 1, "e4m3").T
    U = f64(Z) + f64(e) * G
    th = f64(theta)
    y = U - np.minimum(np.maximum(U, -th), th)
    Y = y.T
    words, scales = planes(Y)
    return y, words, scales

@@ -1,0 +1,420 @@
+from contextlib import ExitStack
+
+import concourse.mybir as mybir
+from concourse.masks import make_identity
+
+T, A, F, BLK = 1024, 2048, 1024, 128
+FLOPS = 4 * T * A * F
+
+F32 = mybir.dt.float32
+BF16 = mybir.dt.bfloat16
+I32 = mybir.dt.int32
+U32 = mybir.dt.uint32
+U8 = mybir.dt.uint8
+FP8 = mybir.dt.float8_e4m3fn
+FP8X4 = mybir.dt.float8_e4m3fn_x4
+ALU = mybir.AluOpType
+ACT = mybir.ActivationFunctionType
+
+P = 128
+PACK = 4
+K = P * PACK
+AG = A // K
+FG = F // K
+TH = T // K
+
+
+def tile_ista_code_update_b11_kernel(tc, Z, c, D_bytes, D_scale, X, w, e, theta, out_0, out_1, out_2):
+    nc = tc.nc
+    with ExitStack() as ctx:
+        keep = ctx.enter_context(tc.tile_pool(name="keep", bufs=1))
+        work = ctx.enter_context(tc.tile_pool(name="work", bufs=2))
+        psum = ctx.enter_context(tc.psum_pool(name="psum", bufs=8))
+
+        def bank():
+            return psum.tile([P, K], F32, name="bank")
+
+        def staged():
+            return work.tile([P, K * PACK], BF16, name="staged", bufs=8, align_bytes=64)
+
+        def copy_on(eng, out, in_):
+            if eng == "V":
+                nc.vector.tensor_copy(out=out, in_=in_)
+            else:
+                nc.scalar.copy(out=out, in_=in_)
+
+        d_raw = {}
+        pools = {}
+        d_scale = keep.tile([P, AG, PACK * (F // BLK)], F32, name="d_scale")
+        small = keep.tile([P, 4, 16], BF16, name="small")
+        raw = {}
+
+        def load_d(g):
+            d_raw[g] = pools["early"].tile([P, PACK, F], U8, name="d_bytes_%d" % g)
+            nc.sync.dma_start(out=d_raw[g][:], in_=D_bytes[g * K:(g + 1) * K, :].rearrange("(p t) f -> p t f", t=PACK))
+
+        def load_rows(key, src, h, g):
+            raw[key] = work.tile([P, PACK, K], BF16, name="raw", bufs=4)
+            nc.sync.dma_start(out=raw[key][:], in_=src[h * K:(h + 1) * K, g * K:(g + 1) * K].rearrange("(j p) k -> p j k", p=P))
+
+        def load_vec(i, vec, groups):
+            nc.sync.dma_start(out=small[:, i, :groups * PACK].rearrange("p (g t) -> p g t", t=PACK),
+                              in_=vec.rearrange("o (g p t) -> p (o g) t", p=P, t=PACK))
+
+        def first_loads():
+            nc.sync.dma_start(out=d_scale[:], in_=D_scale.rearrange("(g p t) b -> p g (t b)", p=P, t=PACK))
+            load_d(0)
+            load_rows(("z", 0), Z, 0, 0)
+            load_vec(0, c, AG)
+            load_d(1)
+            load_rows(("z", 1), Z, 0, 1)
+            load_d(2)
+            load_rows(("z", 2), Z, 0, 2)
+            load_d(3)
+            load_vec(1, e, AG)
+            load_vec(2, theta, AG)
+            load_vec(3, w, FG)
+
+        ident = keep.tile([P, P], F32, name="ident")
+        ident_bf = keep.tile([P, P], BF16, name="ident_bf")
+        warm = keep.tile([P, 16], F32, name="warm")
+
+        def set_up():
+            make_identity(nc, ident[:])
+            make_identity(nc, ident_bf[:])
+            nc.vector.memset(warm[:, 0:1], 0.0)
+            nc.scalar.activation(out=warm[:, 8:9], in_=warm[:, 0:1], func=ACT.Relu)
+
+        REP = 32
+        c_rep = keep.tile([P, AG, REP, PACK], BF16, name="c_rep")
+        e_f = keep.tile([P, 16], F32, name="e_f")
+        th_f = keep.tile([P, 16], F32, name="th_f")
+        nth_f = keep.tile([P, 16], F32, name="nth_f")
+        w_f = keep.tile([P, 8], F32, name="w_f")
+        nw_f = keep.tile([P, 8], F32, name="nw_f")
+
+        def spread_c():
+            nc.vector.tensor_copy(out=c_rep[:], in_=small[:, 0, :].rearrange("p (g t) -> p g t", t=PACK).unsqueeze(2).to_broadcast([P, AG, REP, PACK]))
+
+        def constants():
+            nc.vector.tensor_copy(out=e_f[:], in_=small[:, 1, :])
+            nc.vector.tensor_copy(out=th_f[:], in_=small[:, 2, :])
+            nc.vector.tensor_scalar(out=nth_f[:], in0=small[:, 2, :], scalar1=-1.0, scalar2=None, op0=ALU.mult)
+            nc.vector.tensor_copy(out=w_f[:], in_=small[:, 3, :8])
+            nc.vector.tensor_scalar(out=nw_f[:], in0=small[:, 3, :8], scalar1=-1.0, scalar2=None, op0=ALU.mult)
+
+        quantised = {}
+
+        def quantise(key, src, pool=keep, name=None, bufs=None):
+            name = name or "q_%s_%d_%d" % key
+            codes = pool.tile([P, K], U32, name=name + "_codes", bufs=bufs, align_bytes=64)
+            scales = pool.tile([P, K], U8, name=name + "_scales", bufs=bufs, align_bytes=64)
+            nc.vector.quantize_mx(out=codes[:].bitcast(FP8X4), scales=scales[:], in_=src[:])
+            quantised[key] = (codes, scales)
+
+        def product(out, lhs, cols, rhs, start, stop):
+            nc.tensor.matmul_mx(out=out, lhsT=quantised[lhs][0][:, cols].bitcast(FP8X4), lhsT_scale=quantised[lhs][1][:, cols],
+                                rhs=quantised[rhs][0][:].bitcast(FP8X4), rhs_scale=quantised[rhs][1][:], start=start, stop=stop)
+
+        held = {}
+
+        def turn_pairs(key, src):
+            words = src[:].rearrange("p j k -> p (j k)").bitcast(F32).rearrange("p (j k) -> p j k", j=PACK)
+            banks = []
+            for half in range(2):
+                b = bank()
+                for j in range(2):
+                    for u in range(2):
+                        nc.tensor.transpose(b[:, (2 * j + u) * P:(2 * j + u + 1) * P], words[:, 2 * half + j, u::2], ident[:])
+                banks.append(b)
+            held[key] = banks
+
+        def empty_pairs(key, dst, engs="SS"):
+            banks = held.pop(key)
+            words = dst[:].bitcast(F32).rearrange("p (h j r u) -> p h j r u", h=2, j=2, u=2)
+            for half in range(2):
+                copy_on(engs[half], words[:, half], banks[half][:].rearrange("p (j u r) -> p j r u", j=2, u=2))
+
+        def d_widen(i, eng):
+            g, fg = i % AG, i // AG
+            wide = pools["early"].tile([P, PACK, K], BF16, name="d_wide", bufs=4)
+            for t in range(PACK):
+                for b in range(K // BLK):
+                    blk = fg * (K // BLK) + b
+                    src = d_raw[g][:, t, blk * BLK:(blk + 1) * BLK].bitcast(FP8)
+                    scale = d_scale[:, g, t * (F // BLK) + blk:t * (F // BLK) + blk + 1]
+                    dst = wide[:, t, b * BLK:(b + 1) * BLK]
+                    if eng[t] == "V":
+                        nc.vector.tensor_scalar(out=dst, in0=src, scalar1=scale, scalar2=None, op0=ALU.mult)
+                    else:
+                        nc.scalar.activation(out=dst, in_=src, func=ACT.Copy, scale=scale)
+            held["wide", i] = wide
+
+        def d_weave(i, eng):
+            st = staged()
+            src = held["wide", i][:].rearrange("p t (m s) -> p s m t", s=PACK)
+            dst = st[:].rearrange("p (s m t) -> p s m t", s=PACK, t=PACK)
+            for half in range(2):
+                copy_on(eng[half], dst[:, 2 * half:2 * half + 2], src[:, 2 * half:2 * half + 2])
+            held["d1", i] = st
+
+        def d_weave_pe(i):
+            src = held["wide", i][:].rearrange("p t (m s) -> p s m t", s=PACK)
+            for half in range(2):
+                b = psum.tile([P, 2, K], BF16, name="bank")
+                for k in range(2):
+                    nc.tensor.matmul(b[:, k, :].rearrange("p (m t) -> p m t", t=PACK), lhsT=ident_bf[:], rhs=src[:, 2 * half + k], start=True, stop=True)
+                held["dI", i, half] = b
+
+        def d_weave_out(i, eng):
+            st = staged()
+            for half in range(2):
+                copy_on(eng[half], st[:, half * 2 * K:(half + 1) * 2 * K], held.pop(("dI", i, half))[:].rearrange("p k n -> p (k n)"))
+            held["d1", i] = st
+
+        def d_turn(i):
+            turn_pairs(("dT", i), held["wide", i])
+
+        def d_empty(i, eng="SS"):
+            held["d2", i] = staged()
+            empty_pairs(("dT", i), held["d2", i], eng)
+
+        def d_quant1(i):
+            quantise(("d1", i % AG, i // AG), held.pop(("d1", i)))
+
+        def d_quant2(i):
+            quantise(("d2", i % AG, i // AG), held.pop(("d2", i)))
+
+        z_t = [keep.tile([P, K * PACK], BF16, name="z_t_%d" % j) for j in range(TH * AG)]
+
+        def z_turn(j):
+            turn_pairs(("zT", j), raw.pop(("z", j)))
+
+        def z_empty(j, eng="SS"):
+            empty_pairs(("zT", j), z_t[j], eng)
+
+        def z_gain(j):
+            st = staged()
+            run = REP * PACK
+            gains = c_rep[:, j % AG].rearrange("p r t -> p (r t)").unsqueeze(1).to_broadcast([P, K * PACK // run, run])
+            nc.vector.tensor_tensor(out=st[:].rearrange("p (n r) -> p n r", r=run), in0=z_t[j][:].rearrange("p (n r) -> p n r", r=run), in1=gains, op=ALU.mult)
+            held["v", j] = st
+
+        def z_quant(j):
+            quantise(("v", j // AG, j % AG), held.pop(("v", j)), work, "q_v", 8)
+
+        def x_turn(r):
+            words = raw.pop(("x", r))[:].rearrange("p j k -> p (j k)").bitcast(F32).rearrange("p (j k) -> p j k", j=PACK)
+            for u in range(2):
+                b = bank()
+                for j in range(PACK):
+                    nc.tensor.transpose(b[:, j * P:(j + 1) * P], words[:, j, u::2], ident[:])
+                held["xT", r, u] = b
+
+        def x_weigh(r):
+            fg = r % FG
+            for u in range(2):
+                pairs = held.pop(("xT", r, u))[:].bitcast(BF16).rearrange("p (n e) -> p n e", e=2)
+                for lo in range(2):
+                    s = 2 * u + lo
+                    xw = work.tile([P, K], F32, name="xw", bufs=6)
+                    nc.scalar.activation(out=xw[:], in_=pairs[:, :, lo], func=ACT.Copy, scale=w_f[:, fg * PACK + s:fg * PACK + s + 1])
+                    held["xw", r, s] = xw
+
+        def h_product(r, s, passes=range(AG)):
+            h, fg = divmod(r, FG)
+            if passes[0] == 0:
+                held["h", r, s] = bank()
+            for g in passes:
+                product(held["h", r, s][:], ("d1", g, fg), slice(s * P, (s + 1) * P), ("v", h, g), g == 0, g == AG - 1)
+
+        def r_plane(r, s):
+            fg = r % FG
+            if s == 0:
+                held["rp", r] = staged()
+            nc.vector.scalar_tensor_tensor(out=held["rp", r][:, s * K:(s + 1) * K], in0=held.pop(("h", r, s))[:], scalar=nw_f[:, fg * PACK + s:fg * PACK + s + 1],
+                                           in1=held.pop(("xw", r, s))[:], op0=ALU.mult, op1=ALU.add)
+
+        def weave(dst, src, eng):
+            d = dst[:].rearrange("p (n t) -> p n t", t=PACK)
+            s_ = src[:].rearrange("p (t n) -> p n t", t=PACK)
+            if eng[0] == eng[1]:
+                copy_on(eng[0], d, s_)
+            else:
+                for half in range(2):
+                    cols = slice(half * K // 2, (half + 1) * K // 2)
+                    copy_on(eng[half], d[:, cols], s_[:, cols])
+
+        def r_weave(r, eng):
+            st = staged()
+            weave(st, held.pop(("rp", r)), eng)
+            held["r", r] = st
+
+        def r_quant(r):
+            quantise(("r",) + divmod(r, FG), held.pop(("r", r)), work, "q_r", 4)
+
+        y_scales = [keep.tile([P, AG, K], U8, name="y_scales_%d" % h, align_bytes=64) for h in range(TH)]
+
+        def g_product(n, t):
+            h, g = divmod(n, AG)
+            b = bank()
+            for fg in range(FG):
+                product(b[:], ("d2", g, fg), slice(t * P, (t + 1) * P), ("r", h, fg), fg == 0, fg == FG - 1)
+            held["g", n, t] = b
+
+        def y_step(n, t):
+            g = n % AG
+            if t == 0:
+                held["y", n] = pools["late"].tile([P, PACK * K], F32, name="y_t", bufs=3)
+            z = z_t[n][:].rearrange("p (n t) -> p t n", t=PACK)
+            nc.vector.scalar_tensor_tensor(out=held["y", n][:, t * K:(t + 1) * K], in0=held.pop(("g", n, t))[:], scalar=e_f[:, g * PACK + t:g * PACK + t + 1],
+                                           in1=z[:, t], op0=ALU.mult, op1=ALU.add)
+
+        def y_upper(n, t):
+            g = n % AG
+            up = pools["late"].tile([P, K], F32, name="upper", bufs=4)
+            nc.scalar.activation(out=up[:], in_=held["y", n][:, t * K:(t + 1) * K], func=ACT.Relu, bias=nth_f[:, g * PACK + t:g * PACK + t + 1])
+            held["up", n, t] = up
+
+        def y_shrink(n, t):
+            g = n % AG
+            u = held["y", n][:, t * K:(t + 1) * K]
+            nc.vector.scalar_tensor_tensor(out=u, in0=u, scalar=th_f[:, g * PACK + t:g * PACK + t + 1], in1=held.pop(("up", n, t))[:], op0=ALU.add, op1=ALU.min)
+
+        def y_turn(n, j):
+            b = bank()
+            for t in range(PACK):
+                nc.tensor.transpose(b[:, t * P:(t + 1) * P], held["y", n][:, t * K + j * P:t * K + (j + 1) * P], ident[:])
+            held["yT", n, j] = b
+
+        def y_weave(n, half, eng):
+            if half == 0:
+                held["yb", n] = staged()
+            cols = slice(half * K // 2, (half + 1) * K // 2)
+            copy_on(eng, held["yb", n][:].rearrange("p (n t) -> p n t", t=PACK)[:, cols], held["y", n][:].rearrange("p (t n) -> p n t", t=PACK)[:, cols])
+
+        def y_empty(n, j, eng="S"):
+            h, g = divmod(n, AG)
+            if j % 2 == 0:
+                held["rows", n] = pools["late"].tile([P, 2, K], F32, name="y_rows", bufs=4)
+            rows = held["rows", n]
+            copy_on(eng, rows[:, j % 2].rearrange("p (m t) -> p m t", t=PACK), held.pop(("yT", n, j))[:].rearrange("p (t m) -> p m t", t=PACK))
+            if j % 2 == 1:
+                t0 = h * K + (j - 1) * P
+                nc.sync.dma_start(out=out_0[t0:t0 + 2 * P, g * K:(g + 1) * K].rearrange("(j p) a -> p j a", p=P), in_=rows[:])
+
+        def y_quant(n):
+            h, g = divmod(n, AG)
+            codes = pools["late"].tile([P, K], U32, name="y_codes", bufs=3, align_bytes=64)
+            nc.vector.quantize_mx(out=codes[:].bitcast(FP8X4), scales=y_scales[h][:, g, :], in_=held.pop(("yb", n))[:])
+            nc.sync.dma_start(out=out_1[g, :, h * K:(h + 1) * K, :].rearrange("p m t -> p (m t)").bitcast(I32), in_=codes[:].bitcast(I32))
+            if g == AG - 1:
+                for q in range(4):
+                    nc.sync.dma_start(out=out_2[:, 4 * q:4 * q + 4, h * K:(h + 1) * K].rearrange("g r m -> r g m").bitcast(I32),
+                                      in_=y_scales[h][32 * q:32 * q + 4].bitcast(I32))
+
+        ND, NY = AG * FG, TH * AG
+        Y0 = 13
+        d_at = list(range(ND))
+        z_at = list(range(ND))
+        x_at = [6, 9, 8, 12]
+        y_at = [Y0 + 2 * n for n in range(NY)]
+        h_at = {7: [(0, 0), (0, 1)], 8: [(0, 2), (0, 3)], 11: [(2, 0), (2, 1)], 12: [(2, 2), (2, 3)], 13: [(3, 0)], 14: [(3, 1)], 15: [(3, 2)], 16: [(3, 3)]}
+        x_at = [6, 8, 10, 12]
+
+        def at(starts, step, lag):
+            return [i for i, s0 in enumerate(starts) if s0 + lag == step]
+
+        def emit(step):
+            last = step >= max(y_at) + 4
+            if step == 1:
+                spread_c()
+            if step == 4:
+                constants()
+            for half in range(2):
+                for n in at(y_at, step, 5 + half):
+                    y_empty(n, 2 * half, "V" if last else "S")
+                    y_empty(n, 2 * half + 1)
+            for half in range(2):
+                for n in at(y_at, step, 1 + half):
+                    for t in (2 * half, 2 * half + 1):
+                        y_step(n, t)
+                        y_upper(n, t)
+            if step == 11:
+                for s in range(PACK):
+                    r_plane(1, s)
+                r_weave(1, "VS")
+            for r, s in h_at.get(step - 1, []):
+                r_plane(r, s)
+            for half in range(2):
+                for n in at(y_at, step, 4 + half):
+                    y_turn(n, 2 * half)
+                    y_turn(n, 2 * half + 1)
+            for i in at(d_at, step, 1):
+                d_weave(i, "SS" if i < 7 else "SV")
+            for i in at(d_at, step, 3):
+                d_empty(i)
+            for j in at(z_at, step, 1):
+                z_empty(j)
+            for r in at(x_at, step, 1):
+                x_weigh(r)
+            for i in at(d_at, step, 0):
+                d_widen(i, "VSVS" if i == 0 else "VVVV")
+            for i in at(d_at, step, 2):
+                d_turn(i)
+            for j in at(z_at, step, 0):
+                z_turn(j)
+            for r in at(x_at, step, 0):
+                x_turn(r)
+            for r in at(x_at, step, -1):
+                load_rows(("x", r), X, r // FG, r % FG)
+            for j in at(z_at, step, -2):
+                if j >= 3:
+                    load_rows(("z", j), Z, j // AG, j % AG)
+            if step == 12:
+                r_quant(1)
+            for half in range(2):
+                for n in at(y_at, step, half):
+                    g_product(n, 2 * half)
+                    g_product(n, 2 * half + 1)
+            for half in range(2):
+                for n in at(y_at, step, 2 + half):
+                    y_shrink(n, 2 * half)
+                    y_shrink(n, 2 * half + 1)
+            for half in range(2):
+                for n in at(y_at, step, 4 + half):
+                    y_weave(n, half, "V" if last else "VS"[half])
+            for r, s in h_at.get(step - 2, []):
+                if s == PACK - 1:
+                    r_weave(r, "SS")
+            for i in at(d_at, step, 2):
+                d_quant1(i)
+            for j in at(z_at, step, 2):
+                z_gain(j)
+            for i in at(d_at, step, 4):
+                d_quant2(i)
+            for j in at(z_at, step, 3):
+                z_quant(j)
+            for r, s in h_at.get(step - 3, []):
+                if s == PACK - 1:
+                    r_quant(r)
+            for n in at(y_at, step, 6):
+                y_quant(n)
+            if step == 9:
+                for s in range(PACK):
+                    h_product(1, s, range(AG - 1))
+                for s in range(PACK):
+                    h_product(1, s, range(AG - 1, AG))
+            for r, s in h_at.get(step, []):
+                h_product(r, s)
+
+        with tc.tile_pool(name="early", bufs=1) as early:
+            pools["early"] = early
+            set_up()
+            first_loads()
+            for step in range(Y0 - 2):
+                emit(step)
+        with tc.tile_pool(name="late", bufs=1) as late:
+            pools["late"] = late
+            for step in range(Y0 - 2, max(y_at) + 7):
+                emit(step)

@@ -35,7 +35,7 @@ def tile_ista_code_update_b11_kernel(tc, Z, c, D_bytes, D_scale, X, w, e, theta,
             return psum.tile([P, K], F32, name="bank")
 
         def staged():
-            return work.tile([P, K * PACK], BF16, name="staged", bufs=8, align_bytes=64)
+            return work.tile([P, K * PACK], BF16, name="staged", bufs=12, align_bytes=64)
 
         def copy_on(eng, out, in_):
             if eng == "V":
@@ -51,10 +51,15 @@ def tile_ista_code_update_b11_kernel(tc, Z, c, D_bytes, D_scale, X, w, e, theta,
 
         def load_d(g):
             d_raw[g] = pools["early"].tile([P, PACK, F], U8, name="d_bytes_%d" % g)
-            nc.sync.dma_start(out=d_raw[g][:], in_=D_bytes[g * K:(g + 1) * K, :].rearrange("(p t) f -> p t f", t=PACK))
+            rows = D_bytes[g * K:(g + 1) * K, :].rearrange("(p t) f -> p t f", t=PACK)
+            if g == 0:
+                nc.sync.dma_start(out=d_raw[g][:, :2], in_=rows[:, :2])
+                nc.sync.dma_start(out=d_raw[g][:, 2:], in_=rows[:, 2:])
+            else:
+                nc.sync.dma_start(out=d_raw[g][:], in_=rows)
 
         def load_rows(key, src, h, g):
-            raw[key] = work.tile([P, PACK, K], BF16, name="raw", bufs=4)
+            raw[key] = work.tile([P, PACK, K], BF16, name="raw", bufs=3)
             nc.sync.dma_start(out=raw[key][:], in_=src[h * K:(h + 1) * K, g * K:(g + 1) * K].rearrange("(j p) k -> p j k", p=P))
 
         def load_vec(i, vec, groups):
@@ -65,8 +70,8 @@ def tile_ista_code_update_b11_kernel(tc, Z, c, D_bytes, D_scale, X, w, e, theta,
             nc.sync.dma_start(out=d_scale[:], in_=D_scale.rearrange("(g p t) b -> p g (t b)", p=P, t=PACK))
             load_d(0)
             load_rows(("z", 0), Z, 0, 0)
-            load_vec(0, c, AG)
             load_d(1)
+            load_vec(0, c, AG)
             load_rows(("z", 1), Z, 0, 1)
             load_d(2)
             load_rows(("z", 2), Z, 0, 2)
@@ -112,9 +117,9 @@ def tile_ista_code_update_b11_kernel(tc, Z, c, D_bytes, D_scale, X, w, e, theta,
             nc.vector.quantize_mx(out=codes[:].bitcast(FP8X4), scales=scales[:], in_=src[:])
             quantised[key] = (codes, scales)
 
-        def product(out, lhs, cols, rhs, start, stop):
+        def product(out, lhs, cols, rhs, start, stop, tokens=slice(0, K)):
             nc.tensor.matmul_mx(out=out, lhsT=quantised[lhs][0][:, cols].bitcast(FP8X4), lhsT_scale=quantised[lhs][1][:, cols],
-                                rhs=quantised[rhs][0][:].bitcast(FP8X4), rhs_scale=quantised[rhs][1][:], start=start, stop=stop)
+                                rhs=quantised[rhs][0][:, tokens].bitcast(FP8X4), rhs_scale=quantised[rhs][1][:, tokens], start=start, stop=stop)
 
         held = {}
 
@@ -137,7 +142,7 @@ def tile_ista_code_update_b11_kernel(tc, Z, c, D_bytes, D_scale, X, w, e, theta,
 
         def d_widen(i, eng):
             g, fg = i % AG, i // AG
-            wide = pools["early"].tile([P, PACK, K], BF16, name="d_wide", bufs=4)
+            wide = staged()[:].rearrange("p (t k) -> p t k", t=PACK)
             for t in range(PACK):
                 for b in range(K // BLK):
                     blk = fg * (K // BLK) + b
@@ -152,10 +157,14 @@ def tile_ista_code_update_b11_kernel(tc, Z, c, D_bytes, D_scale, X, w, e, theta,
 
         def d_weave(i, eng):
             st = staged()
-            src = held["wide", i][:].rearrange("p t (m s) -> p s m t", s=PACK)
-            dst = st[:].rearrange("p (s m t) -> p s m t", s=PACK, t=PACK)
-            for half in range(2):
-                copy_on(eng[half], dst[:, 2 * half:2 * half + 2], src[:, 2 * half:2 * half + 2])
+            src = held["wide", i][:].rearrange("p t (m s) -> p m t s", s=PACK)
+            dst = st[:].rearrange("p (s m t) -> p m t s", s=PACK, t=PACK)
+            if eng[0] == eng[1]:
+                copy_on(eng[0], dst, src)
+            else:
+                for half in range(2):
+                    cols = slice(half * P // 2, (half + 1) * P // 2)
+                    copy_on(eng[half], dst[:, cols], src[:, cols])
             held["d1", i] = st
 
         def d_weave_pe(i):
@@ -236,13 +245,13 @@ def tile_ista_code_update_b11_kernel(tc, Z, c, D_bytes, D_scale, X, w, e, theta,
                                            in1=held.pop(("xw", r, s))[:], op0=ALU.mult, op1=ALU.add)
 
         def weave(dst, src, eng):
-            d = dst[:].rearrange("p (n t) -> p n t", t=PACK)
-            s_ = src[:].rearrange("p (t n) -> p n t", t=PACK)
+            d = dst[:].rearrange("p (n i t) -> p n t i", t=PACK, i=PACK)
+            s_ = src[:].rearrange("p (t n i) -> p n t i", t=PACK, i=PACK)
             if eng[0] == eng[1]:
                 copy_on(eng[0], d, s_)
             else:
                 for half in range(2):
-                    cols = slice(half * K // 2, (half + 1) * K // 2)
+                    cols = slice(half * P // 2, (half + 1) * P // 2)
                     copy_on(eng[half], d[:, cols], s_[:, cols])
 
         def r_weave(r, eng):
@@ -255,166 +264,159 @@ def tile_ista_code_update_b11_kernel(tc, Z, c, D_bytes, D_scale, X, w, e, theta,
 
         y_scales = [keep.tile([P, AG, K], U8, name="y_scales_%d" % h, align_bytes=64) for h in range(TH)]
 
-        def g_product(n, t):
+        def g_product(piece, t):
+            n, c0, wd = piece
             h, g = divmod(n, AG)
             b = bank()
             for fg in range(FG):
-                product(b[:], ("d2", g, fg), slice(t * P, (t + 1) * P), ("r", h, fg), fg == 0, fg == FG - 1)
-            held["g", n, t] = b
+                product(b[:, :wd], ("d2", g, fg), slice(t * P, (t + 1) * P), ("r", h, fg), fg == 0, fg == FG - 1, slice(c0, c0 + wd))
+            held["g", piece, t] = b
 
-        def y_step(n, t):
+        def y_step(piece, t):
+            n, c0, wd = piece
             g = n % AG
             if t == 0:
-                held["y", n] = pools["late"].tile([P, PACK * K], F32, name="y_t", bufs=3)
+                held["y", piece] = pools["late"].tile([P, PACK, wd], F32, name="y_t", bufs=3)
             z = z_t[n][:].rearrange("p (n t) -> p t n", t=PACK)
-            nc.vector.scalar_tensor_tensor(out=held["y", n][:, t * K:(t + 1) * K], in0=held.pop(("g", n, t))[:], scalar=e_f[:, g * PACK + t:g * PACK + t + 1],
-                                           in1=z[:, t], op0=ALU.mult, op1=ALU.add)
+            nc.vector.scalar_tensor_tensor(out=held["y", piece][:, t], in0=held.pop(("g", piece, t))[:, :wd], scalar=e_f[:, g * PACK + t:g * PACK + t + 1],
+                                           in1=z[:, t, c0:c0 + wd], op0=ALU.mult, op1=ALU.add)
 
-        def y_upper(n, t):
+        def y_upper(piece, t, eng="S"):
+            n, c0, wd = piece
             g = n % AG
-            up = pools["late"].tile([P, K], F32, name="upper", bufs=4)
-            nc.scalar.activation(out=up[:], in_=held["y", n][:, t * K:(t + 1) * K], func=ACT.Relu, bias=nth_f[:, g * PACK + t:g * PACK + t + 1])
-            held["up", n, t] = up
+            up = pools["late"].tile([P, wd], F32, name="upper", bufs=4)
+            shift = nth_f[:, g * PACK + t:g * PACK + t + 1]
+            if eng == "S":
+                nc.scalar.activation(out=up[:], in_=held["y", piece][:, t], func=ACT.Relu, bias=shift)
+            else:
+                nc.vector.tensor_scalar(out=up[:], in0=held["y", piece][:, t], scalar1=shift, scalar2=0.0, op0=ALU.add, op1=ALU.max)
+            held["up", piece, t] = up
 
-        def y_shrink(n, t):
-            g = n % AG
-            u = held["y", n][:, t * K:(t + 1) * K]
-            nc.vector.scalar_tensor_tensor(out=u, in0=u, scalar=th_f[:, g * PACK + t:g * PACK + t + 1], in1=held.pop(("up", n, t))[:], op0=ALU.add, op1=ALU.min)
+        def y_shrink(piece, t):
+            g = piece[0] % AG
+            u = held["y", piece][:, t]
+            nc.vector.scalar_tensor_tensor(out=u, in0=u, scalar=th_f[:, g * PACK + t:g * PACK + t + 1], in1=held.pop(("up", piece, t))[:], op0=ALU.add, op1=ALU.min)
 
-        def y_turn(n, j):
+        def y_turn(piece, j):
             b = bank()
             for t in range(PACK):
-                nc.tensor.transpose(b[:, t * P:(t + 1) * P], held["y", n][:, t * K + j * P:t * K + (j + 1) * P], ident[:])
-            held["yT", n, j] = b
+                nc.tensor.transpose(b[:, t * P:(t + 1) * P], held["y", piece][:, t, j * P:(j + 1) * P], ident[:])
+            held["yT", piece, j] = b
 
-        def y_weave(n, half, eng):
+        def y_weave(piece, half, eng):
+            wd = piece[2]
             if half == 0:
-                held["yb", n] = staged()
-            cols = slice(half * K // 2, (half + 1) * K // 2)
-            copy_on(eng, held["yb", n][:].rearrange("p (n t) -> p n t", t=PACK)[:, cols], held["y", n][:].rearrange("p (t n) -> p n t", t=PACK)[:, cols])
+                held["yb", piece] = staged()[:, :wd * PACK]
+            cols = slice(half * wd // 8, (half + 1) * wd // 8)
+            copy_on(eng, held["yb", piece].rearrange("p (n i t) -> p n t i", t=PACK, i=PACK)[:, cols], held["y", piece][:].rearrange("p t (n i) -> p n t i", i=PACK)[:, cols])
 
-        def y_empty(n, j, eng="S"):
+        def y_empty(piece, j, eng="S"):
+            n, c0, wd = piece
             h, g = divmod(n, AG)
-            if j % 2 == 0:
-                held["rows", n] = pools["late"].tile([P, 2, K], F32, name="y_rows", bufs=4)
-            rows = held["rows", n]
-            copy_on(eng, rows[:, j % 2].rearrange("p (m t) -> p m t", t=PACK), held.pop(("yT", n, j))[:].rearrange("p (t m) -> p m t", t=PACK))
-            if j % 2 == 1:
-                t0 = h * K + (j - 1) * P
-                nc.sync.dma_start(out=out_0[t0:t0 + 2 * P, g * K:(g + 1) * K].rearrange("(j p) a -> p j a", p=P), in_=rows[:])
+            per = wd // (2 * P)
+            if j % per == 0:
+                held["rows", piece] = pools["late"].tile([P, per, K], F32, name="y_rows", bufs=4)
+            rows = held["rows", piece]
+            copy_on(eng, rows[:, j % per].rearrange("p (m t) -> p m t", t=PACK), held.pop(("yT", piece, j))[:].rearrange("p (t m) -> p m t", t=PACK))
+            if j % per == per - 1:
+                t0 = h * K + c0 + (j - per + 1) * P
+                nc.sync.dma_start(out=out_0[t0:t0 + per * P, g * K:(g + 1) * K].rearrange("(j p) a -> p j a", p=P), in_=rows[:])
 
-        def y_quant(n):
+        def y_quant(piece):
+            n, c0, wd = piece
             h, g = divmod(n, AG)
-            codes = pools["late"].tile([P, K], U32, name="y_codes", bufs=3, align_bytes=64)
-            nc.vector.quantize_mx(out=codes[:].bitcast(FP8X4), scales=y_scales[h][:, g, :], in_=held.pop(("yb", n))[:])
-            nc.sync.dma_start(out=out_1[g, :, h * K:(h + 1) * K, :].rearrange("p m t -> p (m t)").bitcast(I32), in_=codes[:].bitcast(I32))
-            if g == AG - 1:
+            codes = pools["late"].tile([P, wd], U32, name="y_codes", bufs=3, align_bytes=64)
+            nc.vector.quantize_mx(out=codes[:].bitcast(FP8X4), scales=y_scales[h][:, g, c0:c0 + wd], in_=held.pop(("yb", piece)))
+            t0 = h * K + c0
+            nc.sync.dma_start(out=out_1[g, :, t0:t0 + wd, :].rearrange("p m t -> p (m t)").bitcast(I32), in_=codes[:].bitcast(I32))
+            if g == AG - 1 and c0 + wd == K:
                 for q in range(4):
-                    nc.sync.dma_start(out=out_2[:, 4 * q:4 * q + 4, h * K:(h + 1) * K].rearrange("g r m -> r g m").bitcast(I32),
+                    (nc.scalar if h == TH - 1 and q % 2 else nc.sync).dma_start(out=out_2[:, 4 * q:4 * q + 4, h * K:(h + 1) * K].rearrange("g r m -> r g m").bitcast(I32),
                                       in_=y_scales[h][32 * q:32 * q + 4].bitcast(I32))
 
         ND, NY = AG * FG, TH * AG
-        Y0 = 13
-        d_at = list(range(ND))
-        z_at = list(range(ND))
-        x_at = [6, 9, 8, 12]
-        y_at = [Y0 + 2 * n for n in range(NY)]
-        h_at = {7: [(0, 0), (0, 1)], 8: [(0, 2), (0, 3)], 11: [(2, 0), (2, 1)], 12: [(2, 2), (2, 3)], 13: [(3, 0)], 14: [(3, 1)], 15: [(3, 2)], 16: [(3, 3)]}
-        x_at = [6, 8, 10, 12]
+        PAIRS = ((0, 1), (2, 3))
 
-        def at(starts, step, lag):
-            return [i for i, s0 in enumerate(starts) if s0 + lag == step]
-
-        def emit(step):
-            last = step >= max(y_at) + 4
-            if step == 1:
-                spread_c()
-            if step == 4:
-                constants()
-            for half in range(2):
-                for n in at(y_at, step, 5 + half):
-                    y_empty(n, 2 * half, "V" if last else "S")
-                    y_empty(n, 2 * half + 1)
-            for half in range(2):
-                for n in at(y_at, step, 1 + half):
-                    for t in (2 * half, 2 * half + 1):
-                        y_step(n, t)
-                        y_upper(n, t)
-            if step == 11:
-                for s in range(PACK):
-                    r_plane(1, s)
-                r_weave(1, "VS")
-            for r, s in h_at.get(step - 1, []):
-                r_plane(r, s)
-            for half in range(2):
-                for n in at(y_at, step, 4 + half):
-                    y_turn(n, 2 * half)
-                    y_turn(n, 2 * half + 1)
-            for i in at(d_at, step, 1):
-                d_weave(i, "SS" if i < 7 else "SV")
-            for i in at(d_at, step, 3):
-                d_empty(i)
-            for j in at(z_at, step, 1):
-                z_empty(j)
-            for r in at(x_at, step, 1):
-                x_weigh(r)
-            for i in at(d_at, step, 0):
-                d_widen(i, "VSVS" if i == 0 else "VVVV")
-            for i in at(d_at, step, 2):
-                d_turn(i)
-            for j in at(z_at, step, 0):
-                z_turn(j)
-            for r in at(x_at, step, 0):
-                x_turn(r)
-            for r in at(x_at, step, -1):
-                load_rows(("x", r), X, r // FG, r % FG)
-            for j in at(z_at, step, -2):
-                if j >= 3:
-                    load_rows(("z", j), Z, j // AG, j % AG)
-            if step == 12:
-                r_quant(1)
-            for half in range(2):
-                for n in at(y_at, step, half):
-                    g_product(n, 2 * half)
-                    g_product(n, 2 * half + 1)
-            for half in range(2):
-                for n in at(y_at, step, 2 + half):
-                    y_shrink(n, 2 * half)
-                    y_shrink(n, 2 * half + 1)
-            for half in range(2):
-                for n in at(y_at, step, 4 + half):
-                    y_weave(n, half, "V" if last else "VS"[half])
-            for r, s in h_at.get(step - 2, []):
-                if s == PACK - 1:
-                    r_weave(r, "SS")
-            for i in at(d_at, step, 2):
-                d_quant1(i)
-            for j in at(z_at, step, 2):
-                z_gain(j)
-            for i in at(d_at, step, 4):
-                d_quant2(i)
-            for j in at(z_at, step, 3):
-                z_quant(j)
-            for r, s in h_at.get(step - 3, []):
-                if s == PACK - 1:
-                    r_quant(r)
-            for n in at(y_at, step, 6):
-                y_quant(n)
-            if step == 9:
-                for s in range(PACK):
-                    h_product(1, s, range(AG - 1))
-                for s in range(PACK):
-                    h_product(1, s, range(AG - 1, AG))
-            for r, s in h_at.get(step, []):
+        def residual(r, weave_eng):
+            x_turn(r)
+            x_weigh(r)
+            for s in range(PACK):
                 h_product(r, s)
+                r_plane(r, s)
+            r_weave(r, weave_eng)
+            r_quant(r)
+
+        def d_second(g):
+            for fg in range(FG):
+                d_turn(fg * AG + g)
+                d_empty(fg * AG + g)
+                d_quant2(fg * AG + g)
+
+        def codes(j):
+            z_turn(j)
+            z_empty(j)
+            z_gain(j)
+            z_quant(j)
+
+        def update_front(n):
+            for pair in PAIRS:
+                for t in pair:
+                    g_product(n, t)
+                for t in pair:
+                    y_step(n, t)
+                    y_upper(n, t)
+
+        def update_middle(n):
+            for t in range(PACK):
+                y_shrink(n, t)
+
+        def update_back(n, weave_eng, empty_eng):
+            for half in range(2):
+                y_weave(n, half, weave_eng[half])
+            y_quant(n)
+            for j in range(n[2] // P):
+                y_turn(n, j)
+                y_empty(n, j, empty_eng[j])
 
         with tc.tile_pool(name="early", bufs=1) as early:
             pools["early"] = early
             set_up()
             first_loads()
-            for step in range(Y0 - 2):
-                emit(step)
+            spread_c()
+            load_rows(("z", 3), Z, 0, 3)
+            load_rows(("x", 0), X, 0, 0)
+            load_rows(("x", 1), X, 0, 1)
+            for g in range(AG):
+                d_widen(g, "VSVS" if g == 0 else "VVVV")
+                d_weave(g, "SS")
+                codes(g)
+                d_quant1(g)
+            constants()
+            for g in range(AG):
+                d_widen(AG + g, "VVVV")
+                d_weave(AG + g, "VS")
+                d_quant1(AG + g)
+                if g == 1:
+                    residual(0, "SS")
+                load_rows(("z", AG + g), Z, 1, g)
         with tc.tile_pool(name="late", bufs=1) as late:
             pools["late"] = late
-            for step in range(Y0 - 2, max(y_at) + 7):
-                emit(step)
+            residual(1, "VS")
+            d_second(0)
+            for g in range(AG):
+                codes(AG + g)
+            load_rows(("x", 2), X, 1, 0)
+            load_rows(("x", 3), X, 1, 1)
+            pieces = [(n, 0, K) for n in range(NY - 1)] + [(n, c0, K // 2) for n in range(NY - 1, NY) for c0 in (0, K // 2)]
+            NP = len(pieces)
+            for n in range(NP + 2):
+                if n >= 2:
+                    update_back(pieces[n - 2], "VS" if n <= NP else "VV", "SSSS" if n <= NP else "SVSV")
+                if 1 <= n <= NP:
+                    update_middle(pieces[n - 1])
+                if n < NP:
+                    update_front(pieces[n])
+                if n + 1 < AG:
+                    d_second(n + 1)
+                if n in (0, 1):
+                    residual(n + 2, "SS")

@@ -22,6 +22,14 @@ K = P * PACK
 AG = A // K
 FG = F // K
 TH = T // K
+CHUNKS = AG * FG
+BLOCKS = F // BLK
+C_REPEATS = 32
+
+VECTOR, SCALAR = "vector", "scalar"
+SHARED = (VECTOR, SCALAR)
+ALL_SCALAR = (SCALAR, SCALAR)
+ALL_VECTOR = (VECTOR, VECTOR)
 
 
 def tile_ista_code_update_b11_kernel(tc, Z, c, D_bytes, D_scale, X, w, e, theta, out_0, out_1, out_2):
@@ -30,393 +38,431 @@ def tile_ista_code_update_b11_kernel(tc, Z, c, D_bytes, D_scale, X, w, e, theta,
         keep = ctx.enter_context(tc.tile_pool(name="keep", bufs=1))
         work = ctx.enter_context(tc.tile_pool(name="work", bufs=2))
         psum = ctx.enter_context(tc.psum_pool(name="psum", bufs=8))
+        ctx.enter_context(tc.manual_schedule())
+
+        pools = {}
+        held = {}
+        quantised = {}
 
         def bank():
             return psum.tile([P, K], F32, name="bank")
 
         def staged():
-            return work.tile([P, K * PACK], BF16, name="staged", bufs=12, align_bytes=64)
+            return work.tile([P, PACK * K], BF16, name="staged", bufs=12, align_bytes=64)
 
-        def copy_on(eng, out, in_):
-            if eng == "V":
+        def copy_on(engine, out, in_):
+            if engine == VECTOR:
                 nc.vector.tensor_copy(out=out, in_=in_)
             else:
                 nc.scalar.copy(out=out, in_=in_)
 
-        d_raw = {}
-        pools = {}
-        d_scale = keep.tile([P, AG, PACK * (F // BLK)], F32, name="d_scale")
-        small = keep.tile([P, 4, 16], BF16, name="small")
-        raw = {}
+        def copy_halves(engines, out, in_):
+            if engines[0] == engines[1]:
+                copy_on(engines[0], out, in_)
+                return
+            half = out.shape[1] // 2
+            copy_on(engines[0], out[:, :half], in_[:, :half])
+            copy_on(engines[1], out[:, half:], in_[:, half:])
 
-        def load_d(g):
-            d_raw[g] = pools["early"].tile([P, PACK, F], U8, name="d_bytes_%d" % g)
+        def column(tile, group, t):
+            return tile[:, group * PACK + t:group * PACK + t + 1]
+
+        d_scale = keep.tile([P, AG, PACK * BLOCKS], F32, name="d_scale")
+        vectors = keep.tile([P, (3 * AG + FG) * PACK], BF16, name="vectors")
+        per_atom = AG * PACK
+        c_bf, e_bf = vectors[:, :per_atom], vectors[:, per_atom:2 * per_atom]
+        theta_bf, w_bf = vectors[:, 2 * per_atom:3 * per_atom], vectors[:, 3 * per_atom:]
+        ident = keep.tile([P, P], F32, name="ident")
+        warm = keep.tile([P, 16], F32, name="warm")
+        c_runs = keep.tile([P, AG, C_REPEATS, PACK], BF16, name="c_runs")
+        negated = keep.tile([P, (AG + FG) * PACK], F32, name="negated")
+        minus_theta, minus_w = negated[:, :AG * PACK], negated[:, AG * PACK:]
+
+        def load_atoms(g, parts=1):
+            raw = pools["bytes"].tile([P, PACK, F], U8, name="d_bytes_%d" % g)
             rows = D_bytes[g * K:(g + 1) * K, :].rearrange("(p t) f -> p t f", t=PACK)
-            if g == 0:
-                nc.sync.dma_start(out=d_raw[g][:, :2], in_=rows[:, :2])
-                nc.sync.dma_start(out=d_raw[g][:, 2:], in_=rows[:, 2:])
-            else:
-                nc.sync.dma_start(out=d_raw[g][:], in_=rows)
+            for t0 in range(0, PACK, PACK // parts):
+                nc.sync.dma_start(out=raw[:, t0:t0 + PACK // parts], in_=rows[:, t0:t0 + PACK // parts])
+            held["bytes", g] = raw
 
-        def load_rows(key, src, h, g):
-            raw[key] = work.tile([P, PACK, K], BF16, name="raw", bufs=3)
-            nc.sync.dma_start(out=raw[key][:], in_=src[h * K:(h + 1) * K, g * K:(g + 1) * K].rearrange("(j p) k -> p j k", p=P))
+        def load_rows(key, src, h, group):
+            rows = work.tile([P, PACK, K], BF16, name="rows_in", bufs=3)
+            nc.sync.dma_start(out=rows[:], in_=src[h * K:(h + 1) * K, group * K:(group + 1) * K].rearrange("(j p) k -> p j k", p=P))
+            held[key] = rows
 
-        def load_vec(i, vec, groups):
-            nc.sync.dma_start(out=small[:, i, :groups * PACK].rearrange("p (g t) -> p g t", t=PACK),
-                              in_=vec.rearrange("o (g p t) -> p (o g) t", p=P, t=PACK))
+        def load_codes(j):
+            load_rows(("z", j), Z, *divmod(j, AG))
+
+        def load_signals(r):
+            load_rows(("x", r), X, *divmod(r, FG))
+
+        def load_vector(dst, vec):
+            nc.sync.dma_start(out=dst.rearrange("p (g t) -> p g t", t=PACK), in_=vec.rearrange("o (g p t) -> p (o g) t", p=P, t=PACK))
 
         def first_loads():
-            nc.sync.dma_start(out=d_scale[:], in_=D_scale.rearrange("(g p t) b -> p g (t b)", p=P, t=PACK))
-            load_d(0)
-            load_rows(("z", 0), Z, 0, 0)
-            load_d(1)
-            load_vec(0, c, AG)
-            load_rows(("z", 1), Z, 0, 1)
-            load_d(2)
-            load_rows(("z", 2), Z, 0, 2)
-            load_d(3)
-            load_vec(1, e, AG)
-            load_vec(2, theta, AG)
-            load_vec(3, w, FG)
-
-        ident = keep.tile([P, P], F32, name="ident")
-        ident_bf = keep.tile([P, P], BF16, name="ident_bf")
-        warm = keep.tile([P, 16], F32, name="warm")
+            nc.scalar.dma_start(out=d_scale[:], in_=D_scale.rearrange("(g p t) b -> p g (t b)", p=P, t=PACK))
+            load_atoms(0, parts=2)
+            load_codes(0)
+            load_atoms(1)
+            load_vector(c_bf, c)
+            load_codes(1)
+            load_atoms(2)
+            load_codes(2)
+            load_atoms(3)
+            load_vector(e_bf, e)
+            load_vector(theta_bf, theta)
+            load_vector(w_bf, w)
 
         def set_up():
             make_identity(nc, ident[:])
-            make_identity(nc, ident_bf[:])
             nc.vector.memset(warm[:, 0:1], 0.0)
             nc.scalar.activation(out=warm[:, 8:9], in_=warm[:, 0:1], func=ACT.Relu)
 
-        REP = 32
-        c_rep = keep.tile([P, AG, REP, PACK], BF16, name="c_rep")
-        e_f = keep.tile([P, 16], F32, name="e_f")
-        th_f = keep.tile([P, 16], F32, name="th_f")
-        nth_f = keep.tile([P, 16], F32, name="nth_f")
-        w_f = keep.tile([P, 8], F32, name="w_f")
-        nw_f = keep.tile([P, 8], F32, name="nw_f")
+        def spread_gains():
+            gains = c_bf.rearrange("p (g t) -> p g t", t=PACK)
+            nc.vector.tensor_copy(out=c_runs[:], in_=gains.unsqueeze(2).to_broadcast([P, AG, C_REPEATS, PACK]))
 
-        def spread_c():
-            nc.vector.tensor_copy(out=c_rep[:], in_=small[:, 0, :].rearrange("p (g t) -> p g t", t=PACK).unsqueeze(2).to_broadcast([P, AG, REP, PACK]))
+        def negate_theta_and_w():
+            nc.vector.tensor_scalar(out=negated[:], in0=vectors[:, 2 * AG * PACK:], scalar1=-1.0, scalar2=None, op0=ALU.mult)
 
-        def constants():
-            nc.vector.tensor_copy(out=e_f[:], in_=small[:, 1, :])
-            nc.vector.tensor_copy(out=th_f[:], in_=small[:, 2, :])
-            nc.vector.tensor_scalar(out=nth_f[:], in0=small[:, 2, :], scalar1=-1.0, scalar2=None, op0=ALU.mult)
-            nc.vector.tensor_copy(out=w_f[:], in_=small[:, 3, :8])
-            nc.vector.tensor_scalar(out=nw_f[:], in0=small[:, 3, :8], scalar1=-1.0, scalar2=None, op0=ALU.mult)
-
-        quantised = {}
-
-        def quantise(key, src, pool=keep, name=None, bufs=None):
-            name = name or "q_%s_%d_%d" % key
+        def quantise(key, woven, pool, name, bufs):
             codes = pool.tile([P, K], U32, name=name + "_codes", bufs=bufs, align_bytes=64)
             scales = pool.tile([P, K], U8, name=name + "_scales", bufs=bufs, align_bytes=64)
-            nc.vector.quantize_mx(out=codes[:].bitcast(FP8X4), scales=scales[:], in_=src[:])
+            nc.vector.quantize_mx(out=codes[:].bitcast(FP8X4), scales=scales[:], in_=woven[:])
             quantised[key] = (codes, scales)
 
-        def product(out, lhs, cols, rhs, start, stop, tokens=slice(0, K)):
-            nc.tensor.matmul_mx(out=out, lhsT=quantised[lhs][0][:, cols].bitcast(FP8X4), lhsT_scale=quantised[lhs][1][:, cols],
-                                rhs=quantised[rhs][0][:, tokens].bitcast(FP8X4), rhs_scale=quantised[rhs][1][:, tokens], start=start, stop=stop)
+        def mx_pass(out, stationary, t, moving, signals, start, stop):
+            cols = slice(t * P, (t + 1) * P)
+            (lhs, lhs_scale), (rhs, rhs_scale) = quantised[stationary], quantised[moving]
+            nc.tensor.matmul_mx(out=out, lhsT=lhs[:, cols].bitcast(FP8X4), lhsT_scale=lhs_scale[:, cols],
+                                rhs=rhs[:, signals].bitcast(FP8X4), rhs_scale=rhs_scale[:, signals], start=start, stop=stop)
 
-        held = {}
+        def as_pairs(rows):
+            return rows.rearrange("p j k -> p (j k)").bitcast(F32).rearrange("p (j i) -> p j i", j=PACK)
 
-        def turn_pairs(key, src):
-            words = src[:].rearrange("p j k -> p (j k)").bitcast(F32).rearrange("p (j k) -> p j k", j=PACK)
-            banks = []
-            for half in range(2):
+        def turn(key, rows):
+            words = as_pairs(rows)
+            for half in (1, 0):
                 b = bank()
                 for j in range(2):
                     for u in range(2):
                         nc.tensor.transpose(b[:, (2 * j + u) * P:(2 * j + u + 1) * P], words[:, 2 * half + j, u::2], ident[:])
-                banks.append(b)
-            held[key] = banks
+                held[key, half] = b
 
-        def empty_pairs(key, dst, engs="SS"):
-            banks = held.pop(key)
-            words = dst[:].bitcast(F32).rearrange("p (h j r u) -> p h j r u", h=2, j=2, u=2)
+        def empty_turned(key, woven):
+            words = woven[:].bitcast(F32).rearrange("p (half j r u) -> p half j r u", half=2, j=2, u=2)
             for half in range(2):
-                copy_on(engs[half], words[:, half], banks[half][:].rearrange("p (j u r) -> p j r u", j=2, u=2))
+                nc.scalar.copy(out=words[:, half], in_=held.pop((key, half))[:].rearrange("p (j u r) -> p j r u", j=2, u=2))
 
-        def d_widen(i, eng):
-            g, fg = i % AG, i // AG
+        def weave_views(woven, planes):
+            return (woven.rearrange("p (n i t) -> p n t i", t=PACK, i=PACK), planes.rearrange("p t (n i) -> p n t i", i=PACK))
+
+        def d_widen(i, engines=(VECTOR,) * PACK):
+            fg, g = divmod(i, AG)
             wide = staged()[:].rearrange("p (t k) -> p t k", t=PACK)
             for t in range(PACK):
                 for b in range(K // BLK):
-                    blk = fg * (K // BLK) + b
-                    src = d_raw[g][:, t, blk * BLK:(blk + 1) * BLK].bitcast(FP8)
-                    scale = d_scale[:, g, t * (F // BLK) + blk:t * (F // BLK) + blk + 1]
+                    block = fg * (K // BLK) + b
+                    src = held["bytes", g][:, t, block * BLK:(block + 1) * BLK].bitcast(FP8)
+                    scale = d_scale[:, g, t * BLOCKS + block:t * BLOCKS + block + 1]
                     dst = wide[:, t, b * BLK:(b + 1) * BLK]
-                    if eng[t] == "V":
+                    if engines[t] == VECTOR:
                         nc.vector.tensor_scalar(out=dst, in0=src, scalar1=scale, scalar2=None, op0=ALU.mult)
                     else:
                         nc.scalar.activation(out=dst, in_=src, func=ACT.Copy, scale=scale)
-            held["wide", i] = wide
+            held["d_wide", i] = wide
 
-        def d_weave(i, eng):
-            st = staged()
-            src = held["wide", i][:].rearrange("p t (m s) -> p m t s", s=PACK)
-            dst = st[:].rearrange("p (s m t) -> p m t s", s=PACK, t=PACK)
-            if eng[0] == eng[1]:
-                copy_on(eng[0], dst, src)
-            else:
-                for half in range(2):
-                    cols = slice(half * P // 2, (half + 1) * P // 2)
-                    copy_on(eng[half], dst[:, cols], src[:, cols])
-            held["d1", i] = st
+        def d_weave(i, engines):
+            woven = staged()
+            copy_halves(engines, woven[:].rearrange("p (s m t) -> p m t s", s=PACK, t=PACK),
+                        held["d_wide", i].rearrange("p t (m s) -> p m t s", s=PACK))
+            held["d_by_atoms", i] = woven
 
-        def d_weave_pe(i):
-            src = held["wide", i][:].rearrange("p t (m s) -> p s m t", s=PACK)
-            for half in range(2):
-                b = psum.tile([P, 2, K], BF16, name="bank")
-                for k in range(2):
-                    nc.tensor.matmul(b[:, k, :].rearrange("p (m t) -> p m t", t=PACK), lhsT=ident_bf[:], rhs=src[:, 2 * half + k], start=True, stop=True)
-                held["dI", i, half] = b
-
-        def d_weave_out(i, eng):
-            st = staged()
-            for half in range(2):
-                copy_on(eng[half], st[:, half * 2 * K:(half + 1) * 2 * K], held.pop(("dI", i, half))[:].rearrange("p k n -> p (k n)"))
-            held["d1", i] = st
+        def d_quantise_by_atoms(i):
+            quantise(("d_by_atoms", i), held.pop(("d_by_atoms", i)), keep, "d_by_atoms_%d" % i, 1)
 
         def d_turn(i):
-            turn_pairs(("dT", i), held["wide", i])
+            turn(("d_turned", i), held.pop(("d_wide", i)))
 
-        def d_empty(i, eng="SS"):
-            held["d2", i] = staged()
-            empty_pairs(("dT", i), held["d2", i], eng)
+        def d_empty(i):
+            held["d_by_features", i] = staged()
+            empty_turned(("d_turned", i), held["d_by_features", i])
 
-        def d_quant1(i):
-            quantise(("d1", i % AG, i // AG), held.pop(("d1", i)))
+        def d_quantise_by_features(i):
+            quantise(("d_by_features", i), held.pop(("d_by_features", i)), keep, "d_by_features_%d" % i, 1)
 
-        def d_quant2(i):
-            quantise(("d2", i % AG, i // AG), held.pop(("d2", i)))
-
-        z_t = [keep.tile([P, K * PACK], BF16, name="z_t_%d" % j) for j in range(TH * AG)]
+        z_woven = [keep.tile([P, PACK * K], BF16, name="z_woven_%d" % j) for j in range(CHUNKS)]
 
         def z_turn(j):
-            turn_pairs(("zT", j), raw.pop(("z", j)))
+            turn(("z_turned", j), held.pop(("z", j))[:])
 
-        def z_empty(j, eng="SS"):
-            empty_pairs(("zT", j), z_t[j], eng)
+        def z_empty(j):
+            empty_turned(("z_turned", j), z_woven[j])
 
-        def z_gain(j):
-            st = staged()
-            run = REP * PACK
-            gains = c_rep[:, j % AG].rearrange("p r t -> p (r t)").unsqueeze(1).to_broadcast([P, K * PACK // run, run])
-            nc.vector.tensor_tensor(out=st[:].rearrange("p (n r) -> p n r", r=run), in0=z_t[j][:].rearrange("p (n r) -> p n r", r=run), in1=gains, op=ALU.mult)
-            held["v", j] = st
+        def v_product(j):
+            woven = staged()
+            run = C_REPEATS * PACK
+            gains = c_runs[:, j % AG].rearrange("p r t -> p (r t)").unsqueeze(1).to_broadcast([P, PACK * K // run, run])
+            nc.vector.tensor_tensor(out=woven[:].rearrange("p (n r) -> p n r", r=run),
+                                    in0=z_woven[j][:].rearrange("p (n r) -> p n r", r=run), in1=gains, op=ALU.mult)
+            held["v", j] = woven
 
-        def z_quant(j):
-            quantise(("v", j // AG, j % AG), held.pop(("v", j)), work, "q_v", 8)
+        def v_quantise(j):
+            quantise(("v", j), held.pop(("v", j)), work, "v", CHUNKS)
 
         def x_turn(r):
-            words = raw.pop(("x", r))[:].rearrange("p j k -> p (j k)").bitcast(F32).rearrange("p (j k) -> p j k", j=PACK)
-            for u in range(2):
+            words = as_pairs(held.pop(("x", r))[:])
+            for u in (1, 0):
                 b = bank()
                 for j in range(PACK):
                     nc.tensor.transpose(b[:, j * P:(j + 1) * P], words[:, j, u::2], ident[:])
-                held["xT", r, u] = b
+                held["x_turned", r, u] = b
 
         def x_weigh(r):
-            fg = r % FG
             for u in range(2):
-                pairs = held.pop(("xT", r, u))[:].bitcast(BF16).rearrange("p (n e) -> p n e", e=2)
-                for lo in range(2):
-                    s = 2 * u + lo
+                pairs = held.pop(("x_turned", r, u))[:].bitcast(BF16).rearrange("p (n low) -> p n low", low=2)
+                for low in range(2):
                     xw = work.tile([P, K], F32, name="xw", bufs=6)
-                    nc.scalar.activation(out=xw[:], in_=pairs[:, :, lo], func=ACT.Copy, scale=w_f[:, fg * PACK + s:fg * PACK + s + 1])
-                    held["xw", r, s] = xw
+                    nc.scalar.activation(out=xw[:], in_=pairs[:, :, low], func=ACT.Copy, scale=column(minus_w, r % FG, 2 * u + low))
+                    held["xw", r, 2 * u + low] = xw
 
-        def h_product(r, s, passes=range(AG)):
+        def h_passes(r, planes, groups=range(AG)):
             h, fg = divmod(r, FG)
-            if passes[0] == 0:
-                held["h", r, s] = bank()
-            for g in passes:
-                product(held["h", r, s][:], ("d1", g, fg), slice(s * P, (s + 1) * P), ("v", h, g), g == 0, g == AG - 1)
+            for s in planes:
+                if groups[0] == 0:
+                    held["h", r, s] = bank()
+                for g in groups:
+                    mx_pass(held["h", r, s][:], ("d_by_atoms", fg * AG + g), s, ("v", h * AG + g), slice(0, K), g == 0, g == AG - 1)
 
-        def r_plane(r, s):
-            fg = r % FG
-            if s == 0:
-                held["rp", r] = staged()
-            nc.vector.scalar_tensor_tensor(out=held["rp", r][:, s * K:(s + 1) * K], in0=held.pop(("h", r, s))[:], scalar=nw_f[:, fg * PACK + s:fg * PACK + s + 1],
-                                           in1=held.pop(("xw", r, s))[:], op0=ALU.mult, op1=ALU.add)
+        def r_planes(r, planes):
+            if planes[0] == 0:
+                held["r_planes", r] = staged()[:].rearrange("p (t n) -> p t n", t=PACK)
+            for s in planes:
+                nc.vector.scalar_tensor_tensor(out=held["r_planes", r][:, s], in0=held.pop(("h", r, s))[:], scalar=column(minus_w, r % FG, s),
+                                               in1=held.pop(("xw", r, s))[:], op0=ALU.mult, op1=ALU.subtract)
 
-        def weave(dst, src, eng):
-            d = dst[:].rearrange("p (n i t) -> p n t i", t=PACK, i=PACK)
-            s_ = src[:].rearrange("p (t n i) -> p n t i", t=PACK, i=PACK)
-            if eng[0] == eng[1]:
-                copy_on(eng[0], d, s_)
-            else:
-                for half in range(2):
-                    cols = slice(half * P // 2, (half + 1) * P // 2)
-                    copy_on(eng[half], d[:, cols], s_[:, cols])
+        def r_weave(r, engines):
+            woven = staged()
+            copy_halves(engines, *weave_views(woven[:], held.pop(("r_planes", r))))
+            held["r", r] = woven
 
-        def r_weave(r, eng):
-            st = staged()
-            weave(st, held.pop(("rp", r)), eng)
-            held["r", r] = st
-
-        def r_quant(r):
-            quantise(("r",) + divmod(r, FG), held.pop(("r", r)), work, "q_r", 4)
+        def r_quantise(r):
+            quantise(("r", r), held.pop(("r", r)), work, "r", TH * FG)
 
         y_scales = [keep.tile([P, AG, K], U8, name="y_scales_%d" % h, align_bytes=64) for h in range(TH)]
 
-        def g_product(piece, t):
-            n, c0, wd = piece
+        def g_passes(piece, t):
+            n, first, width = piece
             h, g = divmod(n, AG)
             b = bank()
             for fg in range(FG):
-                product(b[:, :wd], ("d2", g, fg), slice(t * P, (t + 1) * P), ("r", h, fg), fg == 0, fg == FG - 1, slice(c0, c0 + wd))
+                mx_pass(b[:, :width], ("d_by_features", fg * AG + g), t, ("r", h * FG + fg), slice(first, first + width), fg == 0, fg == FG - 1)
             held["g", piece, t] = b
 
-        def y_step(piece, t):
-            n, c0, wd = piece
-            g = n % AG
+        def u_plane(piece, t):
+            n, first, width = piece
             if t == 0:
-                held["y", piece] = pools["late"].tile([P, PACK, wd], F32, name="y_t", bufs=3)
-            z = z_t[n][:].rearrange("p (n t) -> p t n", t=PACK)
-            nc.vector.scalar_tensor_tensor(out=held["y", piece][:, t], in0=held.pop(("g", piece, t))[:, :wd], scalar=e_f[:, g * PACK + t:g * PACK + t + 1],
-                                           in1=z[:, t, c0:c0 + wd], op0=ALU.mult, op1=ALU.add)
+                held["y", piece] = pools["update"].tile([P, PACK, width], F32, name="y_planes", bufs=3)
+            z = z_woven[n][:].rearrange("p (n t) -> p t n", t=PACK)[:, t, first:first + width]
+            nc.vector.scalar_tensor_tensor(out=held["y", piece][:, t], in0=held.pop(("g", piece, t))[:, :width],
+                                           scalar=column(e_bf, n % AG, t), in1=z, op0=ALU.mult, op1=ALU.add)
 
-        def y_upper(piece, t, eng="S"):
-            n, c0, wd = piece
-            g = n % AG
-            up = pools["late"].tile([P, wd], F32, name="upper", bufs=4)
-            shift = nth_f[:, g * PACK + t:g * PACK + t + 1]
-            if eng == "S":
-                nc.scalar.activation(out=up[:], in_=held["y", piece][:, t], func=ACT.Relu, bias=shift)
-            else:
-                nc.vector.tensor_scalar(out=up[:], in0=held["y", piece][:, t], scalar1=shift, scalar2=0.0, op0=ALU.add, op1=ALU.max)
-            held["up", piece, t] = up
+        def upper_branch(piece, t):
+            n, first, width = piece
+            upper = pools["update"].tile([P, width], F32, name="upper", bufs=4)
+            nc.scalar.activation(out=upper[:], in_=held["y", piece][:, t], func=ACT.Relu, bias=column(minus_theta, n % AG, t))
+            held["upper", piece, t] = upper
 
-        def y_shrink(piece, t):
-            g = piece[0] % AG
+        def y_plane(piece, t):
             u = held["y", piece][:, t]
-            nc.vector.scalar_tensor_tensor(out=u, in0=u, scalar=th_f[:, g * PACK + t:g * PACK + t + 1], in1=held.pop(("up", piece, t))[:], op0=ALU.add, op1=ALU.min)
+            nc.vector.scalar_tensor_tensor(out=u, in0=u, scalar=column(theta_bf, piece[0] % AG, t),
+                                           in1=held.pop(("upper", piece, t))[:], op0=ALU.add, op1=ALU.min)
 
         def y_turn(piece, j):
             b = bank()
             for t in range(PACK):
                 nc.tensor.transpose(b[:, t * P:(t + 1) * P], held["y", piece][:, t, j * P:(j + 1) * P], ident[:])
-            held["yT", piece, j] = b
+            held["y_turned", piece, j] = b
 
-        def y_weave(piece, half, eng):
-            wd = piece[2]
-            if half == 0:
-                held["yb", piece] = staged()[:, :wd * PACK]
-            cols = slice(half * wd // 8, (half + 1) * wd // 8)
-            copy_on(eng, held["yb", piece].rearrange("p (n i t) -> p n t i", t=PACK, i=PACK)[:, cols], held["y", piece][:].rearrange("p t (n i) -> p n t i", i=PACK)[:, cols])
-
-        def y_empty(piece, j, eng="S"):
-            n, c0, wd = piece
+        def y_store(piece, j, engine):
+            n, first, width = piece
             h, g = divmod(n, AG)
-            per = wd // (2 * P)
-            if j % per == 0:
-                held["rows", piece] = pools["late"].tile([P, per, K], F32, name="y_rows", bufs=4)
-            rows = held["rows", piece]
-            copy_on(eng, rows[:, j % per].rearrange("p (m t) -> p m t", t=PACK), held.pop(("yT", piece, j))[:].rearrange("p (t m) -> p m t", t=PACK))
-            if j % per == per - 1:
-                t0 = h * K + c0 + (j - per + 1) * P
-                nc.sync.dma_start(out=out_0[t0:t0 + per * P, g * K:(g + 1) * K].rearrange("(j p) a -> p j a", p=P), in_=rows[:])
+            if j % 2 == 0:
+                held["rows_out", piece] = pools["update"].tile([P, 2, K], F32, name="rows_out", bufs=4)
+            rows = held["rows_out", piece]
+            copy_on(engine, rows[:, j % 2].rearrange("p (m t) -> p m t", t=PACK),
+                    held.pop(("y_turned", piece, j))[:].rearrange("p (t m) -> p m t", t=PACK))
+            row0 = h * K + first + j * P
+            if width < K:
+                nc.sync.dma_start(out=out_0[row0:row0 + P, g * K:(g + 1) * K], in_=rows[:, j % 2])
+            elif j % 2 == 1:
+                nc.sync.dma_start(out=out_0[row0 - P:row0 + P, g * K:(g + 1) * K].rearrange("(j p) a -> p j a", p=P), in_=rows[:])
 
-        def y_quant(piece):
-            n, c0, wd = piece
+        def y_weave(piece, engines):
+            woven = staged()[:, :piece[2] * PACK]
+            copy_halves(engines, *weave_views(woven, held["y", piece][:]))
+            held["y_woven", piece] = woven
+
+        def y_quantise(piece):
+            n, first, width = piece
             h, g = divmod(n, AG)
-            codes = pools["late"].tile([P, wd], U32, name="y_codes", bufs=3, align_bytes=64)
-            nc.vector.quantize_mx(out=codes[:].bitcast(FP8X4), scales=y_scales[h][:, g, c0:c0 + wd], in_=held.pop(("yb", piece)))
-            t0 = h * K + c0
-            nc.sync.dma_start(out=out_1[g, :, t0:t0 + wd, :].rearrange("p m t -> p (m t)").bitcast(I32), in_=codes[:].bitcast(I32))
-            if g == AG - 1 and c0 + wd == K:
-                for q in range(4):
-                    (nc.scalar if h == TH - 1 and q % 2 else nc.sync).dma_start(out=out_2[:, 4 * q:4 * q + 4, h * K:(h + 1) * K].rearrange("g r m -> r g m").bitcast(I32),
-                                      in_=y_scales[h][32 * q:32 * q + 4].bitcast(I32))
+            codes = pools["update"].tile([P, width], U32, name="y_codes", bufs=4, align_bytes=64)
+            nc.vector.quantize_mx(out=codes[:].bitcast(FP8X4), scales=y_scales[h][:, g, first:first + width], in_=held.pop(("y_woven", piece)))
+            col0 = h * K + first
+            nc.sync.dma_start(out=out_1[g, :, col0:col0 + width, :].rearrange("p m t -> p (m t)").bitcast(I32), in_=codes[:].bitcast(I32))
 
-        ND, NY = AG * FG, TH * AG
-        PAIRS = ((0, 1), (2, 3))
+        def store_scales(h, queues):
+            for q in range(4):
+                queues[q % 2].dma_start(out=out_2[:, 4 * q:4 * q + 4, h * K:(h + 1) * K].rearrange("g r m -> r g m").bitcast(I32),
+                                        in_=y_scales[h][32 * q:32 * q + 4].bitcast(I32))
 
-        def residual(r, weave_eng):
-            x_turn(r)
-            x_weigh(r)
-            for s in range(PACK):
-                h_product(r, s)
-                r_plane(r, s)
-            r_weave(r, weave_eng)
-            r_quant(r)
+        def prepare(step):
+            if step == 1:
+                d_weave(0, SHARED)
+            if step >= 1:
+                z_empty(step - 1)
+            if step >= 2:
+                d_weave(step - 1, SHARED if step - 1 in (2, 4) else ALL_SCALAR)
+            if 2 <= step < AG + 2:
+                d_empty(step - 2)
+            if step == AG + 1:
+                x_weigh(0)
+            d_widen(step, SHARED * 2 if step == 0 else ALL_VECTOR * 2)
+            if step == 1:
+                spread_gains()
+            if step == AG - 1:
+                negate_theta_and_w()
+                load_signals(0)
+            if 1 <= step <= AG:
+                d_turn(step - 1)
+            z_turn(step)
+            if step in (AG, CHUNKS - 1):
+                x_turn(step // (CHUNKS - 1))
+            if step in (AG + 1, AG + 2):
+                h_passes(0, (2 * (step - AG - 1) + 1, 2 * (step - AG - 1)))
+            if 1 <= step < CHUNKS - 2:
+                load_codes(step + 2)
+            if step == CHUNKS - 2:
+                load_signals(1)
+            if step == CHUNKS - 1:
+                h_passes(1, range(PACK), range(AG - 2))
+            if step >= 1:
+                v_product(step - 1)
+            if 2 <= step <= AG:
+                d_quantise_by_atoms(step - 2)
+            if step == 3:
+                d_quantise_by_features(0)
+            if step >= 2 and step != AG + 1:
+                v_quantise(step - 2)
+            if step in (AG + 1, AG + 2):
+                r_planes(0, (2 * (step - AG - 1), 2 * (step - AG - 1) + 1))
+            if step >= AG:
+                d_quantise_by_atoms(step - 1)
+            if step == AG:
+                v_quantise(AG - 1)
 
-        def d_second(g):
-            for fg in range(FG):
-                d_turn(fg * AG + g)
-                d_empty(fg * AG + g)
-                d_quant2(fg * AG + g)
+        def bridge():
+            last = CHUNKS - 1
+            d_weave(last, SHARED)
+            d_quantise_by_atoms(last)
+            h_passes(1, (1, 0, 3, 2), range(AG - 2, AG))
+            z_empty(last)
+            x_weigh(1)
+            d_turn(AG)
+            load_signals(2)
+            r_weave(0, ALL_SCALAR)
+            v_product(last)
+            v_quantise(last - 1)
+            d_empty(AG)
+            d_turn(AG + 1)
+            x_turn(2)
+            load_signals(3)
+            r_planes(1, range(PACK))
+            r_weave(1, SHARED)
+            r_quantise(0)
+            v_quantise(last)
+            h_passes(2, (1, 0))
+            d_empty(AG + 1)
+            x_weigh(2)
+            d_quantise_by_features(AG)
+            r_quantise(1)
+            d_quantise_by_features(1)
+            x_turn(3)
+            r_planes(2, (0, 1))
 
-        def codes(j):
-            z_turn(j)
-            z_empty(j)
-            z_gain(j)
-            z_quant(j)
+        pieces = [(n, 0, K) for n in range(CHUNKS - 1)] + [(CHUNKS - 1, first, K // 2) for first in (0, K // 2)]
+        h_beats = {1: (2, 2), 3: (3, 0), 4: (3, 2)}
 
-        def update_front(n):
-            for pair in PAIRS:
-                for t in pair:
-                    g_product(n, t)
-                for t in pair:
-                    y_step(n, t)
-                    y_upper(n, t)
+        def update(beat):
+            def pair(lag):
+                k = beat - lag
+                return [(pieces[k // 2], 2 * (k % 2), 2 * (k % 2) + 1)] if 0 <= k < 2 * len(pieces) else []
 
-        def update_middle(n):
-            for t in range(PACK):
-                y_shrink(n, t)
+            def blocks(lag):
+                return [(piece, a, b) for piece, a, b in pair(lag) if a < piece[2] // P]
 
-        def update_back(n, weave_eng, empty_eng):
-            for half in range(2):
-                y_weave(n, half, weave_eng[half])
-            y_quant(n)
-            for j in range(n[2] // P):
-                y_turn(n, j)
-                y_empty(n, j, empty_eng[j])
+            for piece, a, b in blocks(5):
+                y_store(piece, a, SCALAR)
+                y_store(piece, b, VECTOR if piece == pieces[-1] else SCALAR)
+            if beat in (2, 3):
+                d_quantise_by_features(beat)
+            for piece, a, b in pair(1):
+                u_plane(piece, a)
+                u_plane(piece, b)
+            if beat - 1 in h_beats:
+                r, s = h_beats[beat - 1]
+                r_planes(r, (s, s + 1))
+            for piece, a, b in pair(4):
+                if a == (2 if piece[2] == K else 0):
+                    y_weave(piece, ALL_SCALAR if piece in pieces[:1] else ALL_VECTOR if piece in pieces[-3:-1] else SHARED)
+            for r in (2, 3):
+                if h_beats.get(beat - 3) == (r, 2):
+                    r_quantise(r)
+            for piece, a, b in pair(1):
+                upper_branch(piece, b)
+                upper_branch(piece, a)
+            for piece, a, b in pair(0):
+                g_passes(piece, b)
+            for piece, a, b in blocks(4):
+                y_turn(piece, b)
+            for piece, a, b in pair(0):
+                g_passes(piece, a)
+            for piece, a, b in blocks(4):
+                y_turn(piece, a)
+            if beat in (2, 4):
+                d_empty(AG + 1 + beat // 2)
+            if beat in h_beats:
+                r, s = h_beats[beat]
+                h_passes(r, (s + 1, s))
+            if beat in (1, 3):
+                d_turn(AG + 2 + beat // 2)
+            if beat == 0:
+                x_weigh(3)
+            for piece, a, b in pair(2):
+                y_plane(piece, a)
+                y_plane(piece, b)
+            if beat in (0, 3, 5):
+                d_quantise_by_features(AG + 1 + beat // 2)
+            for r in (2, 3):
+                if h_beats.get(beat - 2) == (r, 2):
+                    r_weave(r, ALL_SCALAR)
+            for piece, a, b in pair(5):
+                if a == (2 if piece[2] == K else 0) and piece != pieces[-1]:
+                    y_quantise(piece)
+                    if piece[0] == AG - 1:
+                        store_scales(0, (nc.sync, nc.sync))
+            if beat == 2 * len(pieces) + 2:
+                y_quantise(pieces[-1])
 
-        with tc.tile_pool(name="early", bufs=1) as early:
-            pools["early"] = early
-            set_up()
+        with tc.tile_pool(name="bytes", bufs=1) as pool:
+            pools["bytes"] = pool
             first_loads()
-            spread_c()
-            load_rows(("z", 3), Z, 0, 3)
-            load_rows(("x", 0), X, 0, 0)
-            load_rows(("x", 1), X, 0, 1)
-            for g in range(AG):
-                d_widen(g, "VSVS" if g == 0 else "VVVV")
-                d_weave(g, "SS")
-                codes(g)
-                d_quant1(g)
-            constants()
-            for g in range(AG):
-                d_widen(AG + g, "VVVV")
-                d_weave(AG + g, "VS")
-                d_quant1(AG + g)
-                if g == 1:
-                    residual(0, "SS")
-                load_rows(("z", AG + g), Z, 1, g)
-        with tc.tile_pool(name="late", bufs=1) as late:
-            pools["late"] = late
-            residual(1, "VS")
-            d_second(0)
-            for g in range(AG):
-                codes(AG + g)
-            load_rows(("x", 2), X, 1, 0)
-            load_rows(("x", 3), X, 1, 1)
-            pieces = [(n, 0, K) for n in range(NY - 1)] + [(n, c0, K // 2) for n in range(NY - 1, NY) for c0 in (0, K // 2)]
-            NP = len(pieces)
-            for n in range(NP + 2):
-                if n >= 2:
-                    update_back(pieces[n - 2], "VS" if n <= NP else "VV", "SSSS" if n <= NP else "SVSV")
-                if 1 <= n <= NP:
-                    update_middle(pieces[n - 1])
-                if n < NP:
-                    update_front(pieces[n])
-                if n + 1 < AG:
-                    d_second(n + 1)
-                if n in (0, 1):
-                    residual(n + 2, "SS")
+            set_up()
+            for step in range(CHUNKS):
+                prepare(step)
+        with tc.tile_pool(name="update", bufs=1) as pool:
+            pools["update"] = pool
+            bridge()
+            for beat in range(2 * len(pieces) + 4):
+                update(beat)
+            store_scales(1, (nc.sync, nc.scalar))

from contextlib import ExitStack

import concourse.mybir as mybir
from concourse.masks import make_identity

T, A, F, BLK = 1024, 2048, 1024, 128
FLOPS = 4 * T * A * F

F32 = mybir.dt.float32
BF16 = mybir.dt.bfloat16
I32 = mybir.dt.int32
U32 = mybir.dt.uint32
U8 = mybir.dt.uint8
FP8 = mybir.dt.float8_e4m3fn
FP8X4 = mybir.dt.float8_e4m3fn_x4
ALU = mybir.AluOpType
ACT = mybir.ActivationFunctionType

P = 128
PACK = 4
K = P * PACK
AG = A // K
FG = F // K
TH = T // K
CHUNKS = AG * FG
BLOCKS = F // BLK
C_REPEATS = 32

VECTOR, SCALAR = "vector", "scalar"
SHARED = (VECTOR, SCALAR)
ALL_SCALAR = (SCALAR, SCALAR)
ALL_VECTOR = (VECTOR, VECTOR)


def tile_ista_code_update_b11_kernel(tc, Z, c, D_bytes, D_scale, X, w, e, theta, out_0, out_1, out_2):
    nc = tc.nc
    with ExitStack() as ctx:
        keep = ctx.enter_context(tc.tile_pool(name="keep", bufs=1))
        work = ctx.enter_context(tc.tile_pool(name="work", bufs=2))
        psum = ctx.enter_context(tc.psum_pool(name="psum", bufs=8))
        ctx.enter_context(tc.manual_schedule())

        pools = {}
        held = {}
        quantised = {}

        def bank():
            return psum.tile([P, K], F32, name="bank")

        def staged():
            return work.tile([P, PACK * K], BF16, name="staged", bufs=12, align_bytes=64)

        def copy_on(engine, out, in_):
            if engine == VECTOR:
                nc.vector.tensor_copy(out=out, in_=in_)
            else:
                nc.scalar.copy(out=out, in_=in_)

        def copy_halves(engines, out, in_):
            if engines[0] == engines[1]:
                copy_on(engines[0], out, in_)
                return
            half = out.shape[1] // 2
            copy_on(engines[0], out[:, :half], in_[:, :half])
            copy_on(engines[1], out[:, half:], in_[:, half:])

        def column(tile, group, t):
            return tile[:, group * PACK + t:group * PACK + t + 1]

        d_scale = keep.tile([P, AG, PACK * BLOCKS], F32, name="d_scale")
        vectors = keep.tile([P, (3 * AG + FG) * PACK], BF16, name="vectors")
        per_atom = AG * PACK
        c_bf, e_bf = vectors[:, :per_atom], vectors[:, per_atom:2 * per_atom]
        theta_bf, w_bf = vectors[:, 2 * per_atom:3 * per_atom], vectors[:, 3 * per_atom:]
        ident = keep.tile([P, P], F32, name="ident")
        warm = keep.tile([P, 16], F32, name="warm")
        c_runs = keep.tile([P, AG, C_REPEATS, PACK], BF16, name="c_runs")
        negated = keep.tile([P, (AG + FG) * PACK], F32, name="negated")
        minus_theta, minus_w = negated[:, :AG * PACK], negated[:, AG * PACK:]

        def load_atoms(g, parts=1):
            raw = pools["bytes"].tile([P, PACK, F], U8, name="d_bytes_%d" % g)
            rows = D_bytes[g * K:(g + 1) * K, :].rearrange("(p t) f -> p t f", t=PACK)
            for t0 in range(0, PACK, PACK // parts):
                nc.sync.dma_start(out=raw[:, t0:t0 + PACK // parts], in_=rows[:, t0:t0 + PACK // parts])
            held["bytes", g] = raw

        def load_rows(key, src, h, group):
            rows = work.tile([P, PACK, K], BF16, name="rows_in", bufs=3)
            nc.sync.dma_start(out=rows[:], in_=src[h * K:(h + 1) * K, group * K:(group + 1) * K].rearrange("(j p) k -> p j k", p=P))
            held[key] = rows

        def load_codes(j):
            load_rows(("z", j), Z, *divmod(j, AG))

        def load_signals(r):
            load_rows(("x", r), X, *divmod(r, FG))

        def load_vector(dst, vec):
            nc.sync.dma_start(out=dst.rearrange("p (g t) -> p g t", t=PACK), in_=vec.rearrange("o (g p t) -> p (o g) t", p=P, t=PACK))

        def first_loads():
            nc.scalar.dma_start(out=d_scale[:], in_=D_scale.rearrange("(g p t) b -> p g (t b)", p=P, t=PACK))
            load_atoms(0, parts=2)
            load_codes(0)
            load_atoms(1)
            load_vector(c_bf, c)
            load_codes(1)
            load_atoms(2)
            load_codes(2)
            load_atoms(3)
            load_vector(e_bf, e)
            load_vector(theta_bf, theta)
            load_vector(w_bf, w)

        def set_up():
            make_identity(nc, ident[:])
            nc.vector.memset(warm[:, 0:1], 0.0)
            nc.scalar.activation(out=warm[:, 8:9], in_=warm[:, 0:1], func=ACT.Relu)

        def spread_gains():
            gains = c_bf.rearrange("p (g t) -> p g t", t=PACK)
            nc.vector.tensor_copy(out=c_runs[:], in_=gains.unsqueeze(2).to_broadcast([P, AG, C_REPEATS, PACK]))

        def negate_theta_and_w():
            nc.vector.tensor_scalar(out=negated[:], in0=vectors[:, 2 * AG * PACK:], scalar1=-1.0, scalar2=None, op0=ALU.mult)

        def quantise(key, woven, pool, name, bufs):
            codes = pool.tile([P, K], U32, name=name + "_codes", bufs=bufs, align_bytes=64)
            scales = pool.tile([P, K], U8, name=name + "_scales", bufs=bufs, align_bytes=64)
            nc.vector.quantize_mx(out=codes[:].bitcast(FP8X4), scales=scales[:], in_=woven[:])
            quantised[key] = (codes, scales)

        def mx_pass(out, stationary, t, moving, signals, start, stop):
            cols = slice(t * P, (t + 1) * P)
            (lhs, lhs_scale), (rhs, rhs_scale) = quantised[stationary], quantised[moving]
            nc.tensor.matmul_mx(out=out, lhsT=lhs[:, cols].bitcast(FP8X4), lhsT_scale=lhs_scale[:, cols],
                                rhs=rhs[:, signals].bitcast(FP8X4), rhs_scale=rhs_scale[:, signals], start=start, stop=stop)

        def as_pairs(rows):
            return rows.rearrange("p j k -> p (j k)").bitcast(F32).rearrange("p (j i) -> p j i", j=PACK)

        def turn(key, rows):
            words = as_pairs(rows)
            for half in (1, 0):
                b = bank()
                for j in range(2):
                    for u in range(2):
                        nc.tensor.transpose(b[:, (2 * j + u) * P:(2 * j + u + 1) * P], words[:, 2 * half + j, u::2], ident[:])
                held[key, half] = b

        def empty_turned(key, woven):
            words = woven[:].bitcast(F32).rearrange("p (half j r u) -> p half j r u", half=2, j=2, u=2)
            for half in range(2):
                nc.scalar.copy(out=words[:, half], in_=held.pop((key, half))[:].rearrange("p (j u r) -> p j r u", j=2, u=2))

        def weave_views(woven, planes):
            return (woven.rearrange("p (n i t) -> p n t i", t=PACK, i=PACK), planes.rearrange("p t (n i) -> p n t i", i=PACK))

        def d_widen(i, engines=(VECTOR,) * PACK):
            fg, g = divmod(i, AG)
            wide = staged()[:].rearrange("p (t k) -> p t k", t=PACK)
            for t in range(PACK):
                for b in range(K // BLK):
                    block = fg * (K // BLK) + b
                    src = held["bytes", g][:, t, block * BLK:(block + 1) * BLK].bitcast(FP8)
                    scale = d_scale[:, g, t * BLOCKS + block:t * BLOCKS + block + 1]
                    dst = wide[:, t, b * BLK:(b + 1) * BLK]
                    if engines[t] == VECTOR:
                        nc.vector.tensor_scalar(out=dst, in0=src, scalar1=scale, scalar2=None, op0=ALU.mult)
                    else:
                        nc.scalar.activation(out=dst, in_=src, func=ACT.Copy, scale=scale)
            held["d_wide", i] = wide

        def d_weave(i, engines):
            woven = staged()
            copy_halves(engines, woven[:].rearrange("p (s m t) -> p m t s", s=PACK, t=PACK),
                        held["d_wide", i].rearrange("p t (m s) -> p m t s", s=PACK))
            held["d_by_atoms", i] = woven

        def d_quantise_by_atoms(i):
            quantise(("d_by_atoms", i), held.pop(("d_by_atoms", i)), keep, "d_by_atoms_%d" % i, 1)

        def d_turn(i):
            turn(("d_turned", i), held.pop(("d_wide", i)))

        def d_empty(i):
            held["d_by_features", i] = staged()
            empty_turned(("d_turned", i), held["d_by_features", i])

        def d_quantise_by_features(i):
            quantise(("d_by_features", i), held.pop(("d_by_features", i)), keep, "d_by_features_%d" % i, 1)

        z_woven = [keep.tile([P, PACK * K], BF16, name="z_woven_%d" % j) for j in range(CHUNKS)]

        def z_turn(j):
            turn(("z_turned", j), held.pop(("z", j))[:])

        def z_empty(j):
            empty_turned(("z_turned", j), z_woven[j])

        def v_product(j):
            woven = staged()
            run = C_REPEATS * PACK
            gains = c_runs[:, j % AG].rearrange("p r t -> p (r t)").unsqueeze(1).to_broadcast([P, PACK * K // run, run])
            nc.vector.tensor_tensor(out=woven[:].rearrange("p (n r) -> p n r", r=run),
                                    in0=z_woven[j][:].rearrange("p (n r) -> p n r", r=run), in1=gains, op=ALU.mult)
            held["v", j] = woven

        def v_quantise(j):
            quantise(("v", j), held.pop(("v", j)), work, "v", CHUNKS)

        def x_turn(r):
            words = as_pairs(held.pop(("x", r))[:])
            for u in (1, 0):
                b = bank()
                for j in range(PACK):
                    nc.tensor.transpose(b[:, j * P:(j + 1) * P], words[:, j, u::2], ident[:])
                held["x_turned", r, u] = b

        def x_weigh(r):
            for u in range(2):
                pairs = held.pop(("x_turned", r, u))[:].bitcast(BF16).rearrange("p (n low) -> p n low", low=2)
                for low in range(2):
                    xw = work.tile([P, K], F32, name="xw", bufs=6)
                    nc.scalar.activation(out=xw[:], in_=pairs[:, :, low], func=ACT.Copy, scale=column(minus_w, r % FG, 2 * u + low))
                    held["xw", r, 2 * u + low] = xw

        def h_passes(r, planes, groups=range(AG)):
            h, fg = divmod(r, FG)
            for s in planes:
                if groups[0] == 0:
                    held["h", r, s] = bank()
                for g in groups:
                    mx_pass(held["h", r, s][:], ("d_by_atoms", fg * AG + g), s, ("v", h * AG + g), slice(0, K), g == 0, g == AG - 1)

        def r_planes(r, planes):
            if planes[0] == 0:
                held["r_planes", r] = staged()[:].rearrange("p (t n) -> p t n", t=PACK)
            for s in planes:
                nc.vector.scalar_tensor_tensor(out=held["r_planes", r][:, s], in0=held.pop(("h", r, s))[:], scalar=column(minus_w, r % FG, s),
                                               in1=held.pop(("xw", r, s))[:], op0=ALU.mult, op1=ALU.subtract)

        def r_weave(r, engines):
            woven = staged()
            copy_halves(engines, *weave_views(woven[:], held.pop(("r_planes", r))))
            held["r", r] = woven

        def r_quantise(r):
            quantise(("r", r), held.pop(("r", r)), work, "r", TH * FG)

        y_scales = [keep.tile([P, AG, K], U8, name="y_scales_%d" % h, align_bytes=64) for h in range(TH)]

        def g_passes(piece, t):
            n, first, width = piece
            h, g = divmod(n, AG)
            b = bank()
            for fg in range(FG):
                mx_pass(b[:, :width], ("d_by_features", fg * AG + g), t, ("r", h * FG + fg), slice(first, first + width), fg == 0, fg == FG - 1)
            held["g", piece, t] = b

        def u_plane(piece, t):
            n, first, width = piece
            if t == 0:
                held["y", piece] = pools["update"].tile([P, PACK, width], F32, name="y_planes", bufs=3)
            z = z_woven[n][:].rearrange("p (n t) -> p t n", t=PACK)[:, t, first:first + width]
            nc.vector.scalar_tensor_tensor(out=held["y", piece][:, t], in0=held.pop(("g", piece, t))[:, :width],
                                           scalar=column(e_bf, n % AG, t), in1=z, op0=ALU.mult, op1=ALU.add)

        def upper_branch(piece, t):
            n, first, width = piece
            upper = pools["update"].tile([P, width], F32, name="upper", bufs=4)
            nc.scalar.activation(out=upper[:], in_=held["y", piece][:, t], func=ACT.Relu, bias=column(minus_theta, n % AG, t))
            held["upper", piece, t] = upper

        def y_plane(piece, t):
            u = held["y", piece][:, t]
            nc.vector.scalar_tensor_tensor(out=u, in0=u, scalar=column(theta_bf, piece[0] % AG, t),
                                           in1=held.pop(("upper", piece, t))[:], op0=ALU.add, op1=ALU.min)

        def y_turn(piece, j):
            b = bank()
            for t in range(PACK):
                nc.tensor.transpose(b[:, t * P:(t + 1) * P], held["y", piece][:, t, j * P:(j + 1) * P], ident[:])
            held["y_turned", piece, j] = b

        def y_store(piece, j, engine):
            n, first, width = piece
            h, g = divmod(n, AG)
            if j % 2 == 0:
                held["rows_out", piece] = pools["update"].tile([P, 2, K], F32, name="rows_out", bufs=4)
            rows = held["rows_out", piece]
            copy_on(engine, rows[:, j % 2].rearrange("p (m t) -> p m t", t=PACK),
                    held.pop(("y_turned", piece, j))[:].rearrange("p (t m) -> p m t", t=PACK))
            row0 = h * K + first + j * P
            if width < K:
                nc.sync.dma_start(out=out_0[row0:row0 + P, g * K:(g + 1) * K], in_=rows[:, j % 2])
            elif j % 2 == 1:
                nc.sync.dma_start(out=out_0[row0 - P:row0 + P, g * K:(g + 1) * K].rearrange("(j p) a -> p j a", p=P), in_=rows[:])

        def y_weave(piece, engines):
            woven = staged()[:, :piece[2] * PACK]
            copy_halves(engines, *weave_views(woven, held["y", piece][:]))
            held["y_woven", piece] = woven

        def y_quantise(piece):
            n, first, width = piece
            h, g = divmod(n, AG)
            codes = pools["update"].tile([P, width], U32, name="y_codes", bufs=4, align_bytes=64)
            nc.vector.quantize_mx(out=codes[:].bitcast(FP8X4), scales=y_scales[h][:, g, first:first + width], in_=held.pop(("y_woven", piece)))
            col0 = h * K + first
            nc.sync.dma_start(out=out_1[g, :, col0:col0 + width, :].rearrange("p m t -> p (m t)").bitcast(I32), in_=codes[:].bitcast(I32))

        def store_scales(h, queues):
            for q in range(4):
                queues[q % 2].dma_start(out=out_2[:, 4 * q:4 * q + 4, h * K:(h + 1) * K].rearrange("g r m -> r g m").bitcast(I32),
                                        in_=y_scales[h][32 * q:32 * q + 4].bitcast(I32))

        def prepare(step):
            if step == 1:
                d_weave(0, SHARED)
            if step >= 1:
                z_empty(step - 1)
            if step >= 2:
                d_weave(step - 1, SHARED if step - 1 in (2, 4) else ALL_SCALAR)
            if 2 <= step < AG + 2:
                d_empty(step - 2)
            if step == AG + 1:
                x_weigh(0)
            d_widen(step, SHARED * 2 if step == 0 else ALL_VECTOR * 2)
            if step == 1:
                spread_gains()
            if step == AG - 1:
                negate_theta_and_w()
                load_signals(0)
            if 1 <= step <= AG:
                d_turn(step - 1)
            z_turn(step)
            if step in (AG, CHUNKS - 1):
                x_turn(step // (CHUNKS - 1))
            if step in (AG + 1, AG + 2):
                h_passes(0, (2 * (step - AG - 1) + 1, 2 * (step - AG - 1)))
            if 1 <= step < CHUNKS - 2:
                load_codes(step + 2)
            if step == CHUNKS - 2:
                load_signals(1)
            if step == CHUNKS - 1:
                h_passes(1, range(PACK), range(AG - 2))
            if step >= 1:
                v_product(step - 1)
            if 2 <= step <= AG:
                d_quantise_by_atoms(step - 2)
            if step == 3:
                d_quantise_by_features(0)
            if step >= 2 and step != AG + 1:
                v_quantise(step - 2)
            if step in (AG + 1, AG + 2):
                r_planes(0, (2 * (step - AG - 1), 2 * (step - AG - 1) + 1))
            if step >= AG:
                d_quantise_by_atoms(step - 1)
            if step == AG:
                v_quantise(AG - 1)

        def bridge():
            last = CHUNKS - 1
            d_weave(last, SHARED)
            d_quantise_by_atoms(last)
            h_passes(1, (1, 0, 3, 2), range(AG - 2, AG))
            z_empty(last)
            x_weigh(1)
            d_turn(AG)
            load_signals(2)
            r_weave(0, ALL_SCALAR)
            v_product(last)
            v_quantise(last - 1)
            d_empty(AG)
            d_turn(AG + 1)
            x_turn(2)
            load_signals(3)
            r_planes(1, range(PACK))
            r_weave(1, SHARED)
            r_quantise(0)
            v_quantise(last)
            h_passes(2, (1, 0))
            d_empty(AG + 1)
            x_weigh(2)
            d_quantise_by_features(AG)
            r_quantise(1)
            d_quantise_by_features(1)
            x_turn(3)
            r_planes(2, (0, 1))

        pieces = [(n, 0, K) for n in range(CHUNKS - 1)] + [(CHUNKS - 1, first, K // 2) for first in (0, K // 2)]
        h_beats = {1: (2, 2), 3: (3, 0), 4: (3, 2)}

        def update(beat):
            def pair(lag):
                k = beat - lag
                return [(pieces[k // 2], 2 * (k % 2), 2 * (k % 2) + 1)] if 0 <= k < 2 * len(pieces) else []

            def blocks(lag):
                return [(piece, a, b) for piece, a, b in pair(lag) if a < piece[2] // P]

            for piece, a, b in blocks(5):
                y_store(piece, a, SCALAR)
                y_store(piece, b, VECTOR if piece == pieces[-1] else SCALAR)
            if beat in (2, 3):
                d_quantise_by_features(beat)
            for piece, a, b in pair(1):
                u_plane(piece, a)
                u_plane(piece, b)
            if beat - 1 in h_beats:
                r, s = h_beats[beat - 1]
                r_planes(r, (s, s + 1))
            for piece, a, b in pair(4):
                if a == (2 if piece[2] == K else 0):
                    y_weave(piece, ALL_SCALAR if piece in pieces[:1] else ALL_VECTOR if piece in pieces[-3:-1] else SHARED)
            for r in (2, 3):
                if h_beats.get(beat - 3) == (r, 2):
                    r_quantise(r)
            for piece, a, b in pair(1):
                upper_branch(piece, b)
                upper_branch(piece, a)
            for piece, a, b in pair(0):
                g_passes(piece, b)
            for piece, a, b in blocks(4):
                y_turn(piece, b)
            for piece, a, b in pair(0):
                g_passes(piece, a)
            for piece, a, b in blocks(4):
                y_turn(piece, a)
            if beat in (2, 4):
                d_empty(AG + 1 + beat // 2)
            if beat in h_beats:
                r, s = h_beats[beat]
                h_passes(r, (s + 1, s))
            if beat in (1, 3):
                d_turn(AG + 2 + beat // 2)
            if beat == 0:
                x_weigh(3)
            for piece, a, b in pair(2):
                y_plane(piece, a)
                y_plane(piece, b)
            if beat in (0, 3, 5):
                d_quantise_by_features(AG + 1 + beat // 2)
            for r in (2, 3):
                if h_beats.get(beat - 2) == (r, 2):
                    r_weave(r, ALL_SCALAR)
            for piece, a, b in pair(5):
                if a == (2 if piece[2] == K else 0) and piece != pieces[-1]:
                    y_quantise(piece)
                    if piece[0] == AG - 1:
                        store_scales(0, (nc.sync, nc.sync))
            if beat == 2 * len(pieces) + 2:
                y_quantise(pieces[-1])

        with tc.tile_pool(name="bytes", bufs=1) as pool:
            pools["bytes"] = pool
            first_loads()
            set_up()
            for step in range(CHUNKS):
                prepare(step)
        with tc.tile_pool(name="update", bufs=1) as pool:
            pools["update"] = pool
            bridge()
            for beat in range(2 * len(pieces) + 4):
                update(beat)
            store_scales(1, (nc.sync, nc.scalar))
